import numpy as np
import ml_dtypes


def mxq(x, axis, fmt="e4m3"):
    dtype, down = {"e4m3": (ml_dtypes.float8_e4m3fn, 7), "e5m2": (ml_dtypes.float8_e5m2, 14)}[fmt]
    v = np.moveaxis(np.asarray(x, np.float32).astype(ml_dtypes.bfloat16).astype(np.float64), axis, -1)
    blocks = v.reshape(v.shape[:-1] + (-1, 32))
    amax = np.abs(blocks).max(-1, keepdims=True)
    byte = np.maximum(np.where(amax > 0, np.frexp(amax)[1] - 1 + 127, 0) - down, 1)
    scale = np.exp2(byte - 127.0)
    codes = (blocks / scale).astype(np.float32).astype(dtype).astype(np.float64)
    return np.moveaxis((codes * scale).reshape(v.shape), -1, axis)


WIDE = False


def mx_kscale(k):
    if not WIDE:
        return np.ones(k)
    levels = np.array([10, -10, 5, -5, 0])
    if k % 512:
        return np.exp2(np.random.permutation(np.resize(levels, k // 32))).repeat(32)
    a = np.empty((k // 512, 16))
    for p in range(k // 512):
        a[p, :8] = np.random.permutation(np.resize(levels, 8))
        for g in range(8):
            far = levels[np.abs(levels - a[p, g]) >= 10]
            a[p, g + 8] = far[np.random.randint(len(far))]
    return np.exp2(a.ravel()).repeat(32)


def f64(x):
    return np.asarray(x).astype(np.float64)


def striped(idx):
    return np.tile(idx.reshape(-1, 16).T, (8, 1)).astype(np.uint16)


def unstriped(offs):
    return offs[:16].T.reshape(-1).astype(np.int64)


E2M1 = np.array([0.0, 0.5, 1.0, 1.5, 2.0, 3.0, 4.0, 6.0, -0.0, -0.5, -1.0, -1.5, -2.0, -3.0, -4.0, -6.0])


def pack_weight(w, fmt):
    k, n = w.shape
    w = f64(np.asarray(w, np.float32).astype(ml_dtypes.bfloat16)).reshape(k // 32, 32, n)
    amax = np.abs(w).max(1)
    if fmt == "e4m3":
        byte = np.frexp(amax)[1] - 1 + 127 - 7
    else:
        mant, ex = np.frexp(amax / 6.0)
        byte = np.where(mant > 0.5, ex, ex - 1) + 127
    byte = np.clip(np.where(amax > 0, byte, 1), 1, 254)
    scaled = (w * np.exp2(127.0 - byte)[:, None, :]).reshape(k, n).astype(np.float32)
    by_word = np.ascontiguousarray(scaled.reshape(k // 512, 128, 4, n).transpose(0, 1, 3, 2))
    if fmt == "e4m3":
        words = by_word.astype(ml_dtypes.float8_e4m3fn).view(np.uint8)
    else:
        c = by_word.astype(ml_dtypes.float4_e2m1fn).view(np.uint8) & 0xF
        words = (c[..., 0::2] | (c[..., 1::2] << 4)).reshape(k // 512, 128, 2 * n)
    return np.ascontiguousarray(words), np.ascontiguousarray(byte.astype(np.uint8).reshape(k // 512, 16, n))


def unpack_weight(words, scales, fmt):
    g, _, n = scales.shape
    words = np.ascontiguousarray(words).reshape(g, 128, n, -1)
    if fmt == "e4m3":
        vals = words.view(ml_dtypes.float8_e4m3fn).astype(np.float64)
    else:
        nib = np.empty((g, 128, n, 4), np.uint8)
        nib[..., 0::2] = words & 0xF
        nib[..., 1::2] = words >> 4
        vals = E2M1[nib]
    vals = vals * np.repeat(np.exp2(scales.astype(np.float64) - 127.0), 8, axis=1)[..., None]
    return vals.transpose(0, 1, 3, 2).reshape(g * 512, n)


def gelu(v):
    return 0.5 * v * (1.0 + np.tanh(np.sqrt(2.0 / np.pi) * (v + 0.044715 * v**3)))


def twice(P):
    return np.random.permutation(np.repeat(np.arange(P), 2))


def bf(x):
    return np.asarray(x, np.float32).astype(ml_dtypes.bfloat16)


def planes(Y):
    n, m = Y.shape
    b = f64(bf(Y)).reshape(n // 32, 32, m)
    amax = np.abs(b).max(1)
    byte = np.clip(np.where(amax > 0, np.frexp(amax)[1] - 1 + 127 - 7, 1), 1, 254)
    codes = (b * np.exp2(127.0 - byte)[:, None, :]).reshape(n, m).astype(np.float32).astype(ml_dtypes.float8_e4m3fn).view(np.uint8)
    words = codes.reshape(n // 512, 128, 4, m).transpose(0, 1, 3, 2)
    return np.ascontiguousarray(words), np.ascontiguousarray(byte.astype(np.uint8).reshape(n // 512, 16, m))


K, M, H, T, S, P = 1024, 512, 1024, 4096, 1024, 512

def setup_inputs():
    n = np.random.standard_normal
    s = mx_kscale(K)[:, None]
    s1 = mx_kscale(M)[:, None]
    u = mx_kscale(H)[:, None]
    size = np.exp(0.8 * n(H))
    d = {}
    d["tab_words"], d["tab_scales"] = pack_weight(n((K, T)) * s, "e4m3")
    d["offs"] = striped(np.random.permutation(T)[:S])
    d["pos1"] = striped(np.random.permutation(S)[:P])
    d["pos2"] = striped(np.random.permutation(S)[:P])
    d["pos3"] = striped(twice(P))
    d["w1"] = (1.6 * n((K, M)) / K ** 0.5 / s).astype(np.float32)
    d["gain"] = (np.exp(0.3 * n(M)) * s1[:, 0]).astype(np.float32)
    d["w2_words"], d["w2_scales"] = pack_weight(1.3 * n((M, H)) / M ** 0.5 / s1 * u.T, "e4m3")
    d["w3_words"], d["w3_scales"] = pack_weight(0.8 * n((K, H)) / K ** 0.5 / s * u.T, "e2m1")
    d["w4"] = (0.6 * n((H, H)) / H ** 0.5 / u).astype(np.float32)
    d["back"] = (0.7 * size / u[:, 0]).astype(np.float32)
    d["base"] = (0.8 * n((H, S)) * size[:, None]).astype(np.float32)
    return d

def reference(tab_words, tab_scales, offs, pos1, pos2, pos3, w1, gain, w2_words, w2_scales, w3_words, w3_scales, w4, back, base):
    v = unpack_weight(tab_words, tab_scales, "e4m3")[:, unstriped(offs)]
    w2 = unpack_weight(w2_words, w2_scales, "e4m3")
    w3 = unpack_weight(w3_words, w3_scales, "e2m1")
    bent = np.tanh(mxq(f64(w1), 0, "e4m3").T @ v) * f64(gain)[:, None]
    h = w2.T @ mxq(bent, 0, "e4m3") + w3.T @ v
    x = h[:, unstriped(pos1)] - h[:, unstriped(pos2)]
    zone = mxq(f64(w4), 0, "e4m3").T @ mxq(x, 0, "e4m3")
    y = zone[:, unstriped(pos3)] * (h * f64(back)[:, None]) + f64(base)
    words, scales = planes(y)
    return y, words, scales

@@ -1,0 +1,318 @@
+from contextlib import ExitStack
+
+import concourse.mybir as mybir
+
+K, M, H, T, S, Z = 1024, 512, 1024, 4096, 1024, 512
+FLOPS = 2 * (K * M * S + M * H * S + K * H * S + H * H * Z)
+
+F32 = mybir.dt.float32
+BF16 = mybir.dt.bfloat16
+I32 = mybir.dt.int32
+U32 = mybir.dt.uint32
+U16 = mybir.dt.uint16
+U8 = mybir.dt.uint8
+FP8X4 = mybir.dt.float8_e4m3fn_x4
+FP4X4 = mybir.dt.float4_e2m1fn_x4
+ACT = mybir.ActivationFunctionType
+ALU = mybir.AluOpType
+
+P = 128
+PACK = 4
+KP = 512
+BANK = 512
+CH = 128
+SPARE = 16
+
+
+def tile_list_seat_zone_asymmetry_kernel(
+    tc, tab_words, tab_scales, offs, pos1, pos2, pos3, w1, gain, w2_words, w2_scales,
+    w3_words, w3_scales, w4, back, base, out_0, out_1, out_2,
+):
+    nc = tc.nc
+    with ExitStack() as ctx:
+        lists = ctx.enter_context(tc.tile_pool(name="lists", bufs=1))
+        keep = ctx.enter_context(tc.tile_pool(name="keep", bufs=1))
+        stage = ctx.enter_context(tc.tile_pool(name="stage", bufs=2))
+        psum = ctx.enter_context(tc.psum_pool(name="psum", bufs=8))
+
+        def kept(name, shape, dtype):
+            return keep.tile(shape, dtype, name=name, align_bytes=64)
+
+        def staged(name, tag, bufs, shape, dtype):
+            return stage.tile(shape, dtype, name=name, tag=tag, bufs=bufs, align_bytes=64)
+
+        def bank(name):
+            return psum.tile([P, BANK], F32, name=name, tag="bank")
+
+        tab_sc = kept("tab_sc", [P, T], U8)
+        w_sc_raw = kept("w_sc_raw", [P, H], U8)
+        v_sc1 = kept("v_sc1", [P, S], U8)
+        w3_sc1 = kept("w3_sc1", [P, H], U8)
+        for plane in (tab_sc, w_sc_raw, v_sc1, w3_sc1):
+            nc.vector.memset(plane[:].bitcast(I32), 0)
+        zone = [kept("zone%d" % n, [P, Z + SPARE], F32) for n in range(8)]
+        for z in zone:
+            nc.vector.memset(z[:, Z:], 0.0)
+
+        offs_sb = lists.tile([P, S // 16], U16, name="offs_sb")
+        pos1_sb = lists.tile([P, Z // 16], U16, name="pos1_sb")
+        pos2_sb = lists.tile([P, Z // 16], U16, name="pos2_sb")
+        pos3_sb = lists.tile([P, S // 16], U16, name="pos3_sb")
+        nc.sync.dma_start(offs_sb[:], offs)
+        gain_sb = kept("gain_sb", [P, PACK], F32)
+        nc.sync.dma_start(gain_sb[:], gain.rearrange("(p t) -> p t", t=PACK))
+        nc.sync.dma_start(pos2_sb[:], pos2)
+        nc.sync.dma_start(pos1_sb[:], pos1)
+        w3_raw = kept("w3_raw", [P, 2, 2 * H], U8)
+        nc.sync.dma_start(w3_raw[:].bitcast(I32), w3_words.rearrange("a p n -> p a n").bitcast(I32))
+        tab = []
+        for a in range(2):
+            words = staged("tab%d" % a, "big", 2, [P, T], I32)
+            nc.sync.dma_start(words[:], tab_words[a].rearrange("p t i -> p (t i)").bitcast(I32))
+            tab.append(words)
+            if a == 0:
+                for q in range(4):
+                    nc.scalar.dma_start(tab_sc[32 * q : 32 * q + 8, :].bitcast(I32),
+                                        tab_scales[:, 4 * q : 4 * q + 4, :].bitcast(I32))
+        for q in range(4):
+            nc.gpsimd.dma_start(w_sc_raw[32 * q : 32 * q + 8, :].bitcast(I32),
+                                w3_scales[:, 4 * q : 4 * q + 4, :].bitcast(I32))
+        for q in range(4):
+            nc.gpsimd.dma_start(w_sc_raw[32 * q + 8 : 32 * q + 12, :].bitcast(I32),
+                                w2_scales[0, 4 * q : 4 * q + 4, :].bitcast(I32))
+        w1_rows = w1.rearrange("(a p i) m -> a p i m", p=P, i=PACK)
+        w1_raw = [staged("w1_raw%d" % a, "wraw", 4, [P, PACK, KP], F32) for a in range(2)]
+        nc.sync.dma_start(w1_raw[0][:], w1_rows[0])
+        for half in range(2):
+            cols = slice(half * 256, (half + 1) * 256)
+            nc.sync.dma_start(w1_raw[1][:, :, cols], w1_rows[1][:, :, cols])
+        w2_raw = kept("w2_raw", [P, H], I32)
+        nc.sync.dma_start(w2_raw[:], w2_words[0].rearrange("p c i -> p (c i)").bitcast(I32))
+        w4_rows = w4.rearrange("(b p i) n -> b p i n", p=P, i=PACK)
+        w4_raw = {}
+        for g in range(2):
+            for b in range(2):
+                raw = staged("w4_raw%d%d" % (b, g), "wraw", 4, [P, PACK, KP], F32)
+                nc.sync.dma_start(raw[:], w4_rows[b][:, :, g * KP : (g + 1) * KP])
+                w4_raw[b, g] = raw
+        back_sb = kept("back_sb", [P, 2, PACK], F32)
+        nc.sync.dma_start(back_sb[:], back.rearrange("(g p t) -> p g t", p=P, t=PACK))
+        nc.sync.dma_start(pos3_sb[:], pos3)
+
+        w3_c = kept("w3_c", [P, 2, 2 * H], U8)
+        nc.vector.tensor_copy(
+            w3_c[:].rearrange("p a (b t q e) -> p (a b) q t e", b=2, t=PACK, e=2),
+            w3_raw[:].rearrange("p a (b q t e) -> p (a b) q t e", b=2, t=PACK, e=2))
+
+        v_sc = kept("v_sc", [P, S], U8)
+        v_c = [kept("v_c%d" % a, [P, S], U32) for a in range(2)]
+        nc.vector.tensor_copy(v_sc[:], tab_sc[:].indirect(offs_sb[:]))
+        nc.scalar.dma_start(v_sc1[0 : P - 4, :].bitcast(I32), v_sc[4:P, :].bitcast(I32))
+        nc.vector.tensor_copy(v_c[0][:], tab[0][:].bitcast(U32).indirect(offs_sb[:]))
+        w_sc = kept("w_sc", [P, H], U8)
+        nc.vector.tensor_copy(
+            w_sc[:].rearrange("p (b t q) -> p b q t", b=2, t=PACK),
+            w_sc_raw[:].rearrange("p (b q t) -> p b q t", b=2, t=PACK))
+        nc.scalar.dma_start(w3_sc1[0 : P - 4, :].bitcast(I32), w_sc[4:P, :].bitcast(I32))
+        nc.vector.tensor_copy(v_c[1][:], tab[1][:].bitcast(U32).indirect(offs_sb[:]))
+
+        y = []
+        base_rows = base.rearrange("(g p t) j -> g p t j", p=P, t=PACK)
+        for g in range(2):
+            rows = staged("y%d" % g, "big", 2, [P, PACK, S], F32)
+            nc.sync.dma_start(rows[:], base_rows[g])
+            y.append(rows)
+
+        def deal_round(copy, dst, raw, q0, q1):
+            copy(dst[:].rearrange("p (t q i) -> p q i t", t=PACK, i=PACK)[:, q0:q1],
+                 raw[:].rearrange("p i (q t) -> p q i t", t=PACK)[:, q0:q1])
+
+        def quantise(codes, scales, src):
+            nc.vector.quantize_mx(out=codes.bitcast(FP8X4), scales=scales, in_=src)
+
+        w1_c = kept("w1_c", [P, 2, M], U32)
+        w1_sc = kept("w1_sc", [P, 2, M], U8)
+        w1_bf = [staged("w1_bf%d" % a, "bf", 3, [P, PACK * KP], BF16) for a in range(2)]
+        deal_round(nc.scalar.copy, w1_bf[0], w1_raw[0], 0, 64)
+        deal_round(nc.vector.tensor_copy, w1_bf[0], w1_raw[0], 64, 128)
+        deal_round(nc.vector.tensor_copy, w1_bf[1], w1_raw[1], 0, 64)
+        quantise(w1_c[:, 0, :], w1_sc[:, 0, :], w1_bf[0][:])
+        deal_round(nc.vector.tensor_copy, w1_bf[1], w1_raw[1], 64, 128)
+        quantise(w1_c[:, 1, :], w1_sc[:, 1, :], w1_bf[1][:])
+        w2_c = kept("w2_c", [P, H], U32)
+        nc.vector.tensor_copy(
+            w2_c[:].bitcast(I32).rearrange("p (b t q) -> p b q t", b=2, t=PACK),
+            w2_raw[:].rearrange("p (b q t) -> p b q t", b=2, t=PACK))
+
+        n_ch = S // CH
+        pre = [bank("pre%d" % c) for c in range(n_ch)]
+
+        def first_product(c, a):
+            cols = slice(c * CH, (c + 1) * CH)
+            for t in range(PACK):
+                m_cols = slice(t * P, (t + 1) * P)
+                nc.tensor.matmul_mx(
+                    out=pre[c][:, t * CH : (t + 1) * CH],
+                    lhsT=w1_c[:, a, m_cols].bitcast(FP8X4), lhsT_scale=w1_sc[:, a, m_cols],
+                    rhs=v_c[a][:, cols].bitcast(FP8X4), rhs_scale=v_sc[4 * a : P, cols],
+                    start=(a == 0 and t == 0), stop=(a == 1 and t == PACK - 1))
+
+        for c in range(n_ch):
+            first_product(c, 0)
+        bent_c = kept("bent_c", [P, S], U32)
+        bent_sc = kept("bent_sc", [P, S], U8)
+        gain_wide = gain_sb[:].unsqueeze(1).to_broadcast([P, CH, PACK])
+        bent_bf = {}
+
+        def bend(c):
+            first_product(c, 1)
+            th = staged("th%d" % c, "th", 3, [P, CH, PACK], F32)
+            nc.scalar.activation(th[:], pre[c][:].rearrange("p (t n) -> p n t", t=PACK), ACT.Tanh)
+            bent_bf[c] = staged("bent_bf%d" % c, "bent_bf", 3, [P, CH, PACK], BF16)
+            nc.vector.tensor_tensor(bent_bf[c][:], th[:], gain_wide, ALU.mult)
+
+        def quantise_bent(c):
+            cols = slice(c * CH, (c + 1) * CH)
+            quantise(bent_c[:, cols], bent_sc[:, cols], bent_bf[c][:].rearrange("p n t -> p (n t)"))
+
+        for c in range(n_ch):
+            bend(c)
+            if c > 0:
+                quantise_bent(c - 1)
+        quantise_bent(n_ch - 1)
+
+        h = [kept("h%d" % n, [P, S], F32) for n in range(8)]
+        w3_planes = (w_sc, w3_sc1)
+        v_planes = (v_sc, v_sc1)
+        for n in range(8):
+            r_cols = slice(n * P, (n + 1) * P)
+            for half in range(2):
+                cols = slice(half * BANK, (half + 1) * BANK)
+                acc = bank("h_acc%d_%d" % (n, half))
+                for a in range(2):
+                    nc.tensor.matmul_mx(
+                        out=acc[:],
+                        lhsT=w3_c[:, a, 2 * n * P : 2 * (n + 1) * P].bitcast(FP4X4),
+                        lhsT_scale=w3_planes[a][:, r_cols],
+                        rhs=v_c[a][:, cols].bitcast(FP8X4), rhs_scale=v_planes[a][:, cols],
+                        start=(a == 0), stop=False)
+                nc.tensor.matmul_mx(
+                    out=acc[:],
+                    lhsT=w2_c[:, r_cols].bitcast(FP8X4), lhsT_scale=w_sc[8:P, r_cols],
+                    rhs=bent_c[:, cols].bitcast(FP8X4), rhs_scale=bent_sc[:, cols],
+                    start=False, stop=True)
+                nc.scalar.copy(h[n][:, cols], acc[:])
+
+        w4_c = kept("w4_c", [P, 2, H], U32)
+        w4_sc = kept("w4_sc", [P, 2, H], U8)
+        w4_bf = {}
+        for b in range(2):
+            w4_bf[b, 0] = staged("w4_bf%d0" % b, "bf", 3, [P, PACK * KP], BF16)
+            for q0 in range(0, P, 32):
+                deal_round(nc.scalar.copy, w4_bf[b, 0], w4_raw[b, 0], q0, q0 + 32)
+
+        def quantise_w4(b, g):
+            cols = slice(g * KP, (g + 1) * KP)
+            quantise(w4_c[:, b, cols], w4_sc[:, b, cols], w4_bf[b, g][:])
+
+        def interleave_round(copy, dst, src):
+            copy(dst.rearrange("p (c i t) -> p c t i", i=4, t=PACK),
+                 src.rearrange("p t (c i) -> p c t i", i=4))
+
+        x_f = [staged("x_f%d" % b, "x_f", 2, [P, PACK, Z], F32) for b in range(2)]
+        x_c = kept("x_c", [P, 2, Z], U32)
+        x_sc = kept("x_sc", [P, 2, Z], U8)
+        x_bf = {}
+        right = {}
+
+        def pick_right(n):
+            right[n] = staged("right%d" % n, "right", 2, [P, Z], F32)
+            nc.vector.tensor_copy(right[n][:], h[n][:].indirect(pos2_sb[:]))
+
+        def subtract(n):
+            nc.vector.tensor_tensor(x_f[n // PACK][:, n % PACK, :], h[n][:].indirect(pos1_sb[:]),
+                                    right[n][:], ALU.subtract)
+
+        def round_x(b):
+            x_bf[b] = staged("x_bf%d" % b, "bf", 3, [P, PACK * Z], BF16)
+            interleave_round(nc.scalar.copy, x_bf[b][:], x_f[b][:])
+
+        pick_right(0)
+        for n in range(1, 8):
+            pick_right(n)
+            subtract(n - 1)
+            if n == 4:
+                quantise_w4(0, 0)
+                round_x(0)
+            if n == 6:
+                quantise_w4(1, 0)
+                quantise(x_c[:, 0, :], x_sc[:, 0, :], x_bf[0][:])
+        subtract(7)
+        round_x(1)
+        for b in range(2):
+            w4_bf[b, 1] = staged("w4_bf%d1" % b, "right", 2, [P, PACK * KP], BF16)
+            deal_round(nc.vector.tensor_copy, w4_bf[b, 1], w4_raw[b, 1], 0, P)
+        quantise(x_c[:, 1, :], x_sc[:, 1, :], x_bf[1][:])
+        for b in range(2):
+            quantise_w4(b, 1)
+
+        for n in range(8):
+            n_cols = slice(n * P, (n + 1) * P)
+            acc = bank("z_acc%d" % n)
+            for b in range(2):
+                nc.tensor.matmul_mx(
+                    out=acc[:],
+                    lhsT=w4_c[:, b, n_cols].bitcast(FP8X4), lhsT_scale=w4_sc[:, b, n_cols],
+                    rhs=x_c[:, b, :].bitcast(FP8X4), rhs_scale=x_sc[:, b, :],
+                    start=(b == 0), stop=(b == 1))
+            nc.scalar.activation(zone[n][:, 0:Z], acc[:], ACT.Copy,
+                                 scale=back_sb[:, n // PACK, n % PACK : n % PACK + 1])
+
+        out_rows = out_0.rearrange("(g p t) j -> g p t j", p=P, t=PACK)
+        y_c = [kept("y_c%d" % g, [P, S], U32) for g in range(2)]
+        y_sc = [kept("y_sc%d" % g, [P, S], U8) for g in range(2)]
+        pieces = [(0, 0, 512), (0, 512, 512), (1, 0, 512), (1, 512, 256), (1, 768, 256)]
+        steps = [(g, j0, w, t) for g, j0, w in pieces for t in range(PACK)]
+        raised = {}
+        y_bf = {}
+
+        def raise_zone(s):
+            g, j0, w, t = steps[s]
+            n = PACK * g + t
+            raised[s] = staged("raised%d" % s, "raised", 3, [P, w], F32)
+            nc.vector.tensor_tensor(raised[s][:], zone[n][:].indirect(pos3_sb[:, j0 // 16 : (j0 + w) // 16]),
+                                    h[n][:, j0 : j0 + w], ALU.mult)
+
+        def add_base(s):
+            g, j0, w, t = steps[s]
+            dst = y[g][:, t, j0 : j0 + w]
+            nc.vector.tensor_tensor(dst, raised[s][:], dst, ALU.add)
+
+        def finish_rows(k):
+            g, j0, w = pieces[k]
+            cols = slice(j0, j0 + w)
+            nc.sync.dma_start(out_rows[g][:, :, cols], y[g][:, :, cols])
+            y_bf[k] = staged("y_bf%d" % k, "bf", 3, [P, PACK * w], BF16)
+            copy = nc.vector.tensor_copy if k == len(pieces) - 1 else nc.scalar.copy
+            interleave_round(copy, y_bf[k][:], y[g][:, :, cols])
+
+        def finish_planes(k):
+            g, j0, w = pieces[k]
+            cols = slice(j0, j0 + w)
+            quantise(y_c[g][:, cols], y_sc[g][:, cols], y_bf[k][:])
+            nc.sync.dma_start(out_1[g].rearrange("p m t -> p (m t)").bitcast(I32)[:, cols], y_c[g][:, cols].bitcast(I32))
+            if j0 + w == S:
+                for q in range(4):
+                    nc.sync.dma_start(out_2[g, 4 * q : 4 * q + 4, :].bitcast(I32),
+                                      y_sc[g][32 * q : 32 * q + 4, :].bitcast(I32))
+
+        raise_zone(0)
+        for s in range(1, len(steps) + 1):
+            if s < len(steps):
+                raise_zone(s)
+            add_base(s - 1)
+            if s % PACK == 0:
+                finish_rows(s // PACK - 1)
+                if s > PACK:
+                    finish_planes(s // PACK - 2)
+        finish_planes(len(pieces) - 1)

@@ -1,6 +1,7 @@
 from contextlib import ExitStack
 
 import concourse.mybir as mybir
+from concourse.masks import make_identity
 
 K, M, H, T, S, Z = 1024, 512, 1024, 4096, 1024, 512
 FLOPS = 2 * (K * M * S + M * H * S + K * H * S + H * H * Z)
@@ -22,6 +23,7 @@ KP = 512
 BANK = 512
 CH = 128
 SPARE = 16
+SPLIT = 352
 
 
 def tile_list_seat_zone_asymmetry_kernel(
@@ -33,7 +35,7 @@ def tile_list_seat_zone_asymmetry_kernel(
         lists = ctx.enter_context(tc.tile_pool(name="lists", bufs=1))
         keep = ctx.enter_context(tc.tile_pool(name="keep", bufs=1))
         stage = ctx.enter_context(tc.tile_pool(name="stage", bufs=2))
-        psum = ctx.enter_context(tc.psum_pool(name="psum", bufs=8))
+        psum = ctx.enter_context(tc.psum_pool(name="psum", bufs=4))
 
         def kept(name, shape, dtype):
             return keep.tile(shape, dtype, name=name, align_bytes=64)
@@ -41,111 +43,131 @@ def tile_list_seat_zone_asymmetry_kernel(
         def staged(name, tag, bufs, shape, dtype):
             return stage.tile(shape, dtype, name=name, tag=tag, bufs=bufs, align_bytes=64)
 
-        def bank(name):
-            return psum.tile([P, BANK], F32, name=name, tag="bank")
+        def bank(name, tag):
+            return psum.tile([P, BANK], F32, name=name, tag=tag)
 
-        tab_sc = kept("tab_sc", [P, T], U8)
-        w_sc_raw = kept("w_sc_raw", [P, H], U8)
+        tab_sc = staged("tab_sc", "bf", 6, [P, T], U8)
+        w_sc_raw = kept("w_sc_raw", [P, 2, H], U8)
         v_sc1 = kept("v_sc1", [P, S], U8)
-        w3_sc1 = kept("w3_sc1", [P, H], U8)
-        for plane in (tab_sc, w_sc_raw, v_sc1, w3_sc1):
+        for plane in (tab_sc, w_sc_raw):
             nc.vector.memset(plane[:].bitcast(I32), 0)
+        nc.gpsimd.memset(v_sc1[:].bitcast(I32), 0)
+        ident = kept("ident", [P, P], F32)
+        make_identity(nc, ident[:])
         zone = [kept("zone%d" % n, [P, Z + SPARE], F32) for n in range(8)]
         for z in zone:
-            nc.vector.memset(z[:, Z:], 0.0)
+            nc.gpsimd.memset(z[:, Z:], 0.0)
 
         offs_sb = lists.tile([P, S // 16], U16, name="offs_sb")
         pos1_sb = lists.tile([P, Z // 16], U16, name="pos1_sb")
         pos2_sb = lists.tile([P, Z // 16], U16, name="pos2_sb")
         pos3_sb = lists.tile([P, S // 16], U16, name="pos3_sb")
+        w3_raw = [staged("w3_raw%d" % a, "bf", 6, [P, 2 * H], U8) for a in range(2)]
+        for a in range(2):
+            nc.sync.dma_start(w3_raw[a][:].bitcast(I32), w3_words[a].bitcast(I32))
         nc.sync.dma_start(offs_sb[:], offs)
         gain_sb = kept("gain_sb", [P, PACK], F32)
         nc.sync.dma_start(gain_sb[:], gain.rearrange("(p t) -> p t", t=PACK))
         nc.sync.dma_start(pos2_sb[:], pos2)
         nc.sync.dma_start(pos1_sb[:], pos1)
-        w3_raw = kept("w3_raw", [P, 2, 2 * H], U8)
-        nc.sync.dma_start(w3_raw[:].bitcast(I32), w3_words.rearrange("a p n -> p a n").bitcast(I32))
-        tab = []
-        for a in range(2):
-            words = staged("tab%d" % a, "big", 2, [P, T], I32)
-            nc.sync.dma_start(words[:], tab_words[a].rearrange("p t i -> p (t i)").bitcast(I32))
-            tab.append(words)
-            if a == 0:
-                for q in range(4):
-                    nc.scalar.dma_start(tab_sc[32 * q : 32 * q + 8, :].bitcast(I32),
-                                        tab_scales[:, 4 * q : 4 * q + 4, :].bitcast(I32))
-        for q in range(4):
-            nc.gpsimd.dma_start(w_sc_raw[32 * q : 32 * q + 8, :].bitcast(I32),
-                                w3_scales[:, 4 * q : 4 * q + 4, :].bitcast(I32))
-        for q in range(4):
-            nc.gpsimd.dma_start(w_sc_raw[32 * q + 8 : 32 * q + 12, :].bitcast(I32),
-                                w2_scales[0, 4 * q : 4 * q + 4, :].bitcast(I32))
-        w1_rows = w1.rearrange("(a p i) m -> a p i m", p=P, i=PACK)
-        w1_raw = [staged("w1_raw%d" % a, "wraw", 4, [P, PACK, KP], F32) for a in range(2)]
-        nc.sync.dma_start(w1_raw[0][:], w1_rows[0])
-        for half in range(2):
-            cols = slice(half * 256, (half + 1) * 256)
-            nc.sync.dma_start(w1_raw[1][:, :, cols], w1_rows[1][:, :, cols])
-        w2_raw = kept("w2_raw", [P, H], I32)
-        nc.sync.dma_start(w2_raw[:], w2_words[0].rearrange("p c i -> p (c i)").bitcast(I32))
-        w4_rows = w4.rearrange("(b p i) n -> b p i n", p=P, i=PACK)
-        w4_raw = {}
-        for g in range(2):
-            for b in range(2):
-                raw = staged("w4_raw%d%d" % (b, g), "wraw", 4, [P, PACK, KP], F32)
-                nc.sync.dma_start(raw[:], w4_rows[b][:, :, g * KP : (g + 1) * KP])
-                w4_raw[b, g] = raw
-        back_sb = kept("back_sb", [P, 2, PACK], F32)
-        nc.sync.dma_start(back_sb[:], back.rearrange("(g p t) -> p g t", p=P, t=PACK))
         nc.sync.dma_start(pos3_sb[:], pos3)
+        tab = [staged("tab%d" % a, "big", 2, [P, T], I32) for a in range(2)]
+
+        def load_table(a, half):
+            cols = slice(half * T // 2, (half + 1) * T // 2)
+            nc.sync.dma_start(tab[a][:, cols], tab_words[a].rearrange("p t i -> p (t i)").bitcast(I32)[:, cols])
+
+        def load_tab_scales(q):
+            nc.sync.dma_start(tab_sc[32 * q : 32 * q + 8, :].bitcast(I32),
+                              tab_scales[:, 4 * q : 4 * q + 4, :].bitcast(I32))
+
+        def load_w3_scales(q):
+            nc.sync.dma_start(w_sc_raw[32 * q : 32 * q + 4, :, :].bitcast(I32),
+                              w3_scales[:, 4 * q : 4 * q + 4, :].rearrange("a r n -> r a n").bitcast(I32))
+
+        def load_w2_scales(q):
+            nc.sync.dma_start(w_sc_raw[32 * q + 4 : 32 * q + 8, 0, :].bitcast(I32),
+                              w2_scales[0, 4 * q : 4 * q + 4, :].bitcast(I32))
+
+        w1_rows = w1.rearrange("(a p i) m -> a p i m", p=P, i=PACK)
+        w1_raw = [staged("w1_raw%d" % a, "w4_raw", 4, [P, PACK, KP], F32) for a in range(2)]
+        for a in range(2):
+            nc.sync.dma_start(w1_raw[a][:], w1_rows[a])
+        for q in range(4):
+            load_tab_scales(q)
+        load_table(0, 0)
+        load_w3_scales(0)
+        load_w3_scales(1)
+        load_table(0, 1)
+        load_w3_scales(2)
+        load_w3_scales(3)
+        load_w2_scales(0)
+        load_table(1, 0)
+        for q in range(1, 4):
+            load_w2_scales(q)
+        load_table(1, 1)
 
         w3_c = kept("w3_c", [P, 2, 2 * H], U8)
-        nc.vector.tensor_copy(
-            w3_c[:].rearrange("p a (b t q e) -> p (a b) q t e", b=2, t=PACK, e=2),
-            w3_raw[:].rearrange("p a (b q t e) -> p (a b) q t e", b=2, t=PACK, e=2))
-
-        v_sc = kept("v_sc", [P, S], U8)
-        v_c = [kept("v_c%d" % a, [P, S], U32) for a in range(2)]
-        nc.vector.tensor_copy(v_sc[:], tab_sc[:].indirect(offs_sb[:]))
-        nc.scalar.dma_start(v_sc1[0 : P - 4, :].bitcast(I32), v_sc[4:P, :].bitcast(I32))
-        nc.vector.tensor_copy(v_c[0][:], tab[0][:].bitcast(U32).indirect(offs_sb[:]))
-        w_sc = kept("w_sc", [P, H], U8)
-        nc.vector.tensor_copy(
-            w_sc[:].rearrange("p (b t q) -> p b q t", b=2, t=PACK),
-            w_sc_raw[:].rearrange("p (b q t) -> p b q t", b=2, t=PACK))
-        nc.scalar.dma_start(w3_sc1[0 : P - 4, :].bitcast(I32), w_sc[4:P, :].bitcast(I32))
-        nc.vector.tensor_copy(v_c[1][:], tab[1][:].bitcast(U32).indirect(offs_sb[:]))
-
-        y = []
-        base_rows = base.rearrange("(g p t) j -> g p t j", p=P, t=PACK)
-        for g in range(2):
-            rows = staged("y%d" % g, "big", 2, [P, PACK, S], F32)
-            nc.sync.dma_start(rows[:], base_rows[g])
-            y.append(rows)
+        for a in range(2):
+            nc.vector.tensor_copy(
+                w3_c[:, a, :].rearrange("p (b t q e) -> p b q t e", b=2, t=PACK, e=2),
+                w3_raw[a][:].rearrange("p (b q t e) -> p b q t e", b=2, t=PACK, e=2))
 
         def deal_round(copy, dst, raw, q0, q1):
             copy(dst[:].rearrange("p (t q i) -> p q i t", t=PACK, i=PACK)[:, q0:q1],
-                 raw[:].rearrange("p i (q t) -> p q i t", t=PACK)[:, q0:q1])
+                 raw.rearrange("p i (q t) -> p q i t", t=PACK)[:, q0:q1])
 
         def quantise(codes, scales, src):
             nc.vector.quantize_mx(out=codes.bitcast(FP8X4), scales=scales, in_=src)
 
         w1_c = kept("w1_c", [P, 2, M], U32)
         w1_sc = kept("w1_sc", [P, 2, M], U8)
-        w1_bf = [staged("w1_bf%d" % a, "bf", 3, [P, PACK * KP], BF16) for a in range(2)]
-        deal_round(nc.scalar.copy, w1_bf[0], w1_raw[0], 0, 64)
-        deal_round(nc.vector.tensor_copy, w1_bf[0], w1_raw[0], 64, 128)
-        deal_round(nc.vector.tensor_copy, w1_bf[1], w1_raw[1], 0, 64)
+        w1_bf = [staged("w1_bf%d" % a, "bf", 6, [P, PACK * KP], BF16) for a in range(2)]
+        for a in range(2):
+            deal_round(nc.scalar.copy, w1_bf[a], w1_raw[a][:], 0, P)
+
+        v_sc = kept("v_sc", [P, S], U8)
+        v_c = [kept("v_c%d" % a, [P, S], U32) for a in range(2)]
         quantise(w1_c[:, 0, :], w1_sc[:, 0, :], w1_bf[0][:])
-        deal_round(nc.vector.tensor_copy, w1_bf[1], w1_raw[1], 64, 128)
+        nc.vector.tensor_copy(v_sc[:], tab_sc[:].indirect(offs_sb[:]))
+        nc.sync.dma_start(v_sc1[0 : P - 4, :].bitcast(I32), v_sc[4:P, :].bitcast(I32))
         quantise(w1_c[:, 1, :], w1_sc[:, 1, :], w1_bf[1][:])
+        nc.vector.tensor_copy(v_c[0][:], tab[0][:].bitcast(U32).indirect(offs_sb[:]))
+        w_sc = kept("w_sc", [P, 2, H], U8)
+        for a in (1, 0):
+            nc.vector.tensor_copy(
+                w_sc[:, a, :].rearrange("p (b t q) -> p b q t", b=2, t=PACK),
+                w_sc_raw[:, a, :].rearrange("p (b q t) -> p b q t", b=2, t=PACK))
+        for half in range(2):
+            nc.vector.tensor_copy(v_c[1][:, half * 512 : (half + 1) * 512],
+                                  tab[1][:].bitcast(U32).indirect(offs_sb[:, half * 32 : (half + 1) * 32]))
+        w2_raw = staged("w2_raw", "bf", 6, [P, H], I32)
+        nc.sync.dma_start(w2_raw[:], w2_words[0].rearrange("p c i -> p (c i)").bitcast(I32))
         w2_c = kept("w2_c", [P, H], U32)
         nc.vector.tensor_copy(
             w2_c[:].bitcast(I32).rearrange("p (b t q) -> p b q t", b=2, t=PACK),
             w2_raw[:].rearrange("p (b q t) -> p b q t", b=2, t=PACK))
+        w4_rows = w4.rearrange("(b p i) n -> b p i n", p=P, i=PACK)
+        w4_raw = {}
+        for g in range(2):
+            for b in range(2):
+                raw = staged("w4_raw%d%d" % (b, g), "w4_raw", 4, [P, PACK, KP], F32)
+                nc.sync.dma_start(raw[:], w4_rows[b][:, :, g * KP : (g + 1) * KP])
+                w4_raw[b, g] = raw[:]
+        back_sb = kept("back_sb", [P, 2, PACK], F32)
+        nc.sync.dma_start(back_sb[:], back.rearrange("(g p t) -> p g t", p=P, t=PACK))
+        base_rows = base.rearrange("(g p t) j -> g p t j", p=P, t=PACK)
+        y = []
+
+        def load_base(g):
+            rows = staged("y%d" % g, "big", 2, [P, PACK, S], F32)
+            nc.sync.dma_start(rows[:], base_rows[g])
+            y.append(rows)
+
+        load_base(0)
 
         n_ch = S // CH
-        pre = [bank("pre%d" % c) for c in range(n_ch)]
+        pre = [bank("pre%d" % c, "ab"[c % 2]) for c in range(n_ch)]
 
         def first_product(c, a):
             cols = slice(c * CH, (c + 1) * CH)
@@ -157,14 +179,13 @@ def tile_list_seat_zone_asymmetry_kernel(
                     rhs=v_c[a][:, cols].bitcast(FP8X4), rhs_scale=v_sc[4 * a : P, cols],
                     start=(a == 0 and t == 0), stop=(a == 1 and t == PACK - 1))
 
-        for c in range(n_ch):
-            first_product(c, 0)
         bent_c = kept("bent_c", [P, S], U32)
         bent_sc = kept("bent_sc", [P, S], U8)
         gain_wide = gain_sb[:].unsqueeze(1).to_broadcast([P, CH, PACK])
         bent_bf = {}
 
         def bend(c):
+            first_product(c, 0)
             first_product(c, 1)
             th = staged("th%d" % c, "th", 3, [P, CH, PACK], F32)
             nc.scalar.activation(th[:], pre[c][:].rearrange("p (t n) -> p n t", t=PACK), ACT.Tanh)
@@ -182,38 +203,39 @@ def tile_list_seat_zone_asymmetry_kernel(
         quantise_bent(n_ch - 1)
 
         h = [kept("h%d" % n, [P, S], F32) for n in range(8)]
-        w3_planes = (w_sc, w3_sc1)
         v_planes = (v_sc, v_sc1)
         for n in range(8):
             r_cols = slice(n * P, (n + 1) * P)
             for half in range(2):
                 cols = slice(half * BANK, (half + 1) * BANK)
-                acc = bank("h_acc%d_%d" % (n, half))
+                acc = bank("h_acc%d_%d" % (n, half), "ab"[half])
                 for a in range(2):
                     nc.tensor.matmul_mx(
                         out=acc[:],
                         lhsT=w3_c[:, a, 2 * n * P : 2 * (n + 1) * P].bitcast(FP4X4),
-                        lhsT_scale=w3_planes[a][:, r_cols],
+                        lhsT_scale=w_sc[:, a, r_cols],
                         rhs=v_c[a][:, cols].bitcast(FP8X4), rhs_scale=v_planes[a][:, cols],
                         start=(a == 0), stop=False)
                 nc.tensor.matmul_mx(
                     out=acc[:],
-                    lhsT=w2_c[:, r_cols].bitcast(FP8X4), lhsT_scale=w_sc[8:P, r_cols],
+                    lhsT=w2_c[:, r_cols].bitcast(FP8X4), lhsT_scale=w_sc[4:P, 0, r_cols],
                     rhs=bent_c[:, cols].bitcast(FP8X4), rhs_scale=bent_sc[:, cols],
                     start=False, stop=True)
                 nc.scalar.copy(h[n][:, cols], acc[:])
 
-        w4_c = kept("w4_c", [P, 2, H], U32)
+        w4_c = {(b, 0): kept("w4_c%d" % b, [P, KP], U32) for b in range(2)}
         w4_sc = kept("w4_sc", [P, 2, H], U8)
         w4_bf = {}
-        for b in range(2):
-            w4_bf[b, 0] = staged("w4_bf%d0" % b, "bf", 3, [P, PACK * KP], BF16)
-            for q0 in range(0, P, 32):
-                deal_round(nc.scalar.copy, w4_bf[b, 0], w4_raw[b, 0], q0, q0 + 32)
+        for g in range(2):
+            for b in range(2):
+                w4_bf[b, g] = staged("w4_bf%d%d" % (b, g), "bf", 6, [P, PACK * KP], BF16)
+                for q0 in range(0, P, 32):
+                    deal_round(nc.scalar.copy, w4_bf[b, g], w4_raw[b, g], q0, q0 + 32)
+            if g == 0:
+                load_base(1)
 
         def quantise_w4(b, g):
-            cols = slice(g * KP, (g + 1) * KP)
-            quantise(w4_c[:, b, cols], w4_sc[:, b, cols], w4_bf[b, g][:])
+            quantise(w4_c[b, g][:], w4_sc[:, b, g * KP : (g + 1) * KP], w4_bf[b, g][:])
 
         def interleave_round(copy, dst, src):
             copy(dst.rearrange("p (c i t) -> p c t i", i=4, t=PACK),
@@ -234,7 +256,7 @@ def tile_list_seat_zone_asymmetry_kernel(
                                     right[n][:], ALU.subtract)
 
         def round_x(b):
-            x_bf[b] = staged("x_bf%d" % b, "bf", 3, [P, PACK * Z], BF16)
+            x_bf[b] = staged("x_bf%d" % b, "bf", 6, [P, PACK * Z], BF16)
             interleave_round(nc.scalar.copy, x_bf[b][:], x_f[b][:])
 
         pick_right(0)
@@ -248,21 +270,22 @@ def tile_list_seat_zone_asymmetry_kernel(
                 quantise_w4(1, 0)
                 quantise(x_c[:, 0, :], x_sc[:, 0, :], x_bf[0][:])
         subtract(7)
-        round_x(1)
-        for b in range(2):
-            w4_bf[b, 1] = staged("w4_bf%d1" % b, "right", 2, [P, PACK * KP], BF16)
-            deal_round(nc.vector.tensor_copy, w4_bf[b, 1], w4_raw[b, 1], 0, P)
+        x_bf[1] = staged("x_bf1", "bf", 6, [P, PACK * Z], BF16)
+        interleave_round(nc.scalar.copy, x_bf[1][:, PACK * SPLIT :], x_f[1][:, :, SPLIT:])
+        interleave_round(nc.vector.tensor_copy, x_bf[1][:, : PACK * SPLIT], x_f[1][:, :, :SPLIT])
         quantise(x_c[:, 1, :], x_sc[:, 1, :], x_bf[1][:])
         for b in range(2):
+            w4_c[b, 1] = staged("w4_c%d1" % b, "right", 2, [P, KP], U32)
             quantise_w4(b, 1)
 
         for n in range(8):
             n_cols = slice(n * P, (n + 1) * P)
-            acc = bank("z_acc%d" % n)
+            acc = bank("z_acc%d" % n, "a")
             for b in range(2):
                 nc.tensor.matmul_mx(
                     out=acc[:],
-                    lhsT=w4_c[:, b, n_cols].bitcast(FP8X4), lhsT_scale=w4_sc[:, b, n_cols],
+                    lhsT=w4_c[b, n // PACK][:, (n % PACK) * P : (n % PACK + 1) * P].bitcast(FP8X4),
+                    lhsT_scale=w4_sc[:, b, n_cols],
                     rhs=x_c[:, b, :].bitcast(FP8X4), rhs_scale=x_sc[:, b, :],
                     start=(b == 0), stop=(b == 1))
             nc.scalar.activation(zone[n][:, 0:Z], acc[:], ACT.Copy,
@@ -279,20 +302,36 @@ def tile_list_seat_zone_asymmetry_kernel(
         def raise_zone(s):
             g, j0, w, t = steps[s]
             n = PACK * g + t
-            raised[s] = staged("raised%d" % s, "raised", 3, [P, w], F32)
+            raised[s] = staged("raised%d" % s, "raised", 5, [P, w], F32)
             nc.vector.tensor_tensor(raised[s][:], zone[n][:].indirect(pos3_sb[:, j0 // 16 : (j0 + w) // 16]),
                                     h[n][:, j0 : j0 + w], ALU.mult)
 
         def add_base(s):
             g, j0, w, t = steps[s]
             dst = y[g][:, t, j0 : j0 + w]
-            nc.vector.tensor_tensor(dst, raised[s][:], dst, ALU.add)
+            if g == 1:
+                nc.vector.tensor_tensor(dst, raised[s][:], dst, ALU.add)
+                return
+            blocks = [slice(k * P, (k + 1) * P) for k in range(w // P)]
+            turned = bank("turned%d" % s, "b")
+            for k, blk in enumerate(blocks):
+                nc.tensor.matmul(turned[:, blk], dst[:, blk], ident[:], is_transpose=True,
+                                 start=(k == 0), stop=False)
+            for k, blk in enumerate(blocks):
+                nc.tensor.matmul(turned[:, blk], raised[s][:, blk], ident[:], is_transpose=True,
+                                 start=False, stop=(k == len(blocks) - 1))
+            summed = staged("summed%d" % s, "summed", 3, [P, w], F32)
+            nc.scalar.copy(summed[:], turned[:])
+            upright = bank("upright%d" % s, "a")
+            for blk in blocks:
+                nc.tensor.transpose(upright[:, blk], summed[:, blk], ident[:])
+            nc.scalar.copy(dst, upright[:])
 
         def finish_rows(k):
             g, j0, w = pieces[k]
             cols = slice(j0, j0 + w)
             nc.sync.dma_start(out_rows[g][:, :, cols], y[g][:, :, cols])
-            y_bf[k] = staged("y_bf%d" % k, "bf", 3, [P, PACK * w], BF16)
+            y_bf[k] = staged("y_bf%d" % k, "bf", 6, [P, PACK * w], BF16)
             copy = nc.vector.tensor_copy if k == len(pieces) - 1 else nc.scalar.copy
             interleave_round(copy, y_bf[k][:], y[g][:, :, cols])
 
@@ -303,8 +342,9 @@ def tile_list_seat_zone_asymmetry_kernel(
             nc.sync.dma_start(out_1[g].rearrange("p m t -> p (m t)").bitcast(I32)[:, cols], y_c[g][:, cols].bitcast(I32))
             if j0 + w == S:
                 for q in range(4):
-                    nc.sync.dma_start(out_2[g, 4 * q : 4 * q + 4, :].bitcast(I32),
-                                      y_sc[g][32 * q : 32 * q + 4, :].bitcast(I32))
+                    queue = nc.scalar if g == 1 and q % 2 == 0 else nc.sync
+                    queue.dma_start(out_2[g, 4 * q : 4 * q + 4, :].bitcast(I32),
+                                    y_sc[g][32 * q : 32 * q + 4, :].bitcast(I32))
 
         raise_zone(0)
         for s in range(1, len(steps) + 1):

@@ -24,6 +24,7 @@ BANK = 512
 CH = 128
 SPARE = 16
 SPLIT = 352
+TURNED_STEPS = 11
 
 
 def tile_list_seat_zone_asymmetry_kernel(
@@ -46,7 +47,7 @@ def tile_list_seat_zone_asymmetry_kernel(
         def bank(name, tag):
             return psum.tile([P, BANK], F32, name=name, tag=tag)
 
-        tab_sc = staged("tab_sc", "bf", 6, [P, T], U8)
+        tab_sc = staged("tab_sc", "bf", 5, [P, T], U8)
         w_sc_raw = kept("w_sc_raw", [P, 2, H], U8)
         v_sc1 = kept("v_sc1", [P, S], U8)
         for plane in (tab_sc, w_sc_raw):
@@ -62,7 +63,7 @@ def tile_list_seat_zone_asymmetry_kernel(
         pos1_sb = lists.tile([P, Z // 16], U16, name="pos1_sb")
         pos2_sb = lists.tile([P, Z // 16], U16, name="pos2_sb")
         pos3_sb = lists.tile([P, S // 16], U16, name="pos3_sb")
-        w3_raw = [staged("w3_raw%d" % a, "bf", 6, [P, 2 * H], U8) for a in range(2)]
+        w3_raw = [staged("w3_raw%d" % a, "bf", 5, [P, 2 * H], U8) for a in range(2)]
         for a in range(2):
             nc.sync.dma_start(w3_raw[a][:].bitcast(I32), w3_words[a].bitcast(I32))
         nc.sync.dma_start(offs_sb[:], offs)
@@ -110,19 +111,19 @@ def tile_list_seat_zone_asymmetry_kernel(
         w3_c = kept("w3_c", [P, 2, 2 * H], U8)
         for a in range(2):
             nc.vector.tensor_copy(
-                w3_c[:, a, :].rearrange("p (b t q e) -> p b q t e", b=2, t=PACK, e=2),
-                w3_raw[a][:].rearrange("p (b q t e) -> p b q t e", b=2, t=PACK, e=2))
+                w3_c[:, a, :].bitcast(U16).rearrange("p (b t q) -> p b t q", b=2, t=PACK),
+                w3_raw[a][:].bitcast(U16).rearrange("p (b q t) -> p b t q", b=2, t=PACK))
 
         def deal_round(copy, dst, raw, q0, q1):
-            copy(dst[:].rearrange("p (t q i) -> p q i t", t=PACK, i=PACK)[:, q0:q1],
-                 raw.rearrange("p i (q t) -> p q i t", t=PACK)[:, q0:q1])
+            copy(dst[:].rearrange("p (t u e i) -> p u i e t", t=PACK, e=2, i=PACK)[:, q0 // 2 : q1 // 2],
+                 raw.rearrange("p i (u e t) -> p u i e t", t=PACK, e=2)[:, q0 // 2 : q1 // 2])
 
         def quantise(codes, scales, src):
             nc.vector.quantize_mx(out=codes.bitcast(FP8X4), scales=scales, in_=src)
 
         w1_c = kept("w1_c", [P, 2, M], U32)
         w1_sc = kept("w1_sc", [P, 2, M], U8)
-        w1_bf = [staged("w1_bf%d" % a, "bf", 6, [P, PACK * KP], BF16) for a in range(2)]
+        w1_bf = [staged("w1_bf%d" % a, "bf", 5, [P, PACK * KP], BF16) for a in range(2)]
         for a in range(2):
             deal_round(nc.scalar.copy, w1_bf[a], w1_raw[a][:], 0, P)
 
@@ -136,12 +137,12 @@ def tile_list_seat_zone_asymmetry_kernel(
         w_sc = kept("w_sc", [P, 2, H], U8)
         for a in (1, 0):
             nc.vector.tensor_copy(
-                w_sc[:, a, :].rearrange("p (b t q) -> p b q t", b=2, t=PACK),
-                w_sc_raw[:, a, :].rearrange("p (b q t) -> p b q t", b=2, t=PACK))
+                w_sc[:, a, :].rearrange("p (b t q) -> p b t q", b=2, t=PACK),
+                w_sc_raw[:, a, :].rearrange("p (b q t) -> p b t q", b=2, t=PACK))
         for half in range(2):
             nc.vector.tensor_copy(v_c[1][:, half * 512 : (half + 1) * 512],
                                   tab[1][:].bitcast(U32).indirect(offs_sb[:, half * 32 : (half + 1) * 32]))
-        w2_raw = staged("w2_raw", "bf", 6, [P, H], I32)
+        w2_raw = staged("w2_raw", "bf", 5, [P, H], I32)
         nc.sync.dma_start(w2_raw[:], w2_words[0].rearrange("p c i -> p (c i)").bitcast(I32))
         w2_c = kept("w2_c", [P, H], U32)
         nc.vector.tensor_copy(
@@ -179,63 +180,78 @@ def tile_list_seat_zone_asymmetry_kernel(
                     rhs=v_c[a][:, cols].bitcast(FP8X4), rhs_scale=v_sc[4 * a : P, cols],
                     start=(a == 0 and t == 0), stop=(a == 1 and t == PACK - 1))
 
-        bent_c = kept("bent_c", [P, S], U32)
+        bent_c = staged("bent_c", "late", 1, [P, S], U32)
         bent_sc = kept("bent_sc", [P, S], U8)
-        gain_wide = gain_sb[:].unsqueeze(1).to_broadcast([P, CH, PACK])
+        runs = [(0, 2), (2, 2), (4, 2), (6, 1), (7, 1)]
         bent_bf = {}
 
-        def bend(c):
-            first_product(c, 0)
-            first_product(c, 1)
-            th = staged("th%d" % c, "th", 3, [P, CH, PACK], F32)
-            nc.scalar.activation(th[:], pre[c][:].rearrange("p (t n) -> p n t", t=PACK), ACT.Tanh)
-            bent_bf[c] = staged("bent_bf%d" % c, "bent_bf", 3, [P, CH, PACK], BF16)
-            nc.vector.tensor_tensor(bent_bf[c][:], th[:], gain_wide, ALU.mult)
+        def bend(k):
+            c0, count = runs[k]
+            th = staged("th%d" % k, "th", 3, [P, count * CH, PACK], F32)
+            for c in range(c0, c0 + count):
+                first_product(c, 0)
+                first_product(c, 1)
+                nc.scalar.activation(th[:, (c - c0) * CH : (c - c0 + 1) * CH, :],
+                                     pre[c][:].rearrange("p (t n) -> p n t", t=PACK), ACT.Tanh)
+            bent_bf[k] = staged("bent_bf%d" % k, "bent_bf", 2, [P, count * CH, PACK], BF16)
+            nc.vector.tensor_tensor(bent_bf[k][:], th[:],
+                                    gain_sb[:].unsqueeze(1).to_broadcast([P, count * CH, PACK]), ALU.mult)
 
-        def quantise_bent(c):
-            cols = slice(c * CH, (c + 1) * CH)
-            quantise(bent_c[:, cols], bent_sc[:, cols], bent_bf[c][:].rearrange("p n t -> p (n t)"))
+        def quantise_bent(k):
+            c0, count = runs[k]
+            cols = slice(c0 * CH, (c0 + count) * CH)
+            quantise(bent_c[:, cols], bent_sc[:, cols], bent_bf[k][:].rearrange("p n t -> p (n t)"))
 
-        for c in range(n_ch):
-            bend(c)
-            if c > 0:
-                quantise_bent(c - 1)
-        quantise_bent(n_ch - 1)
+        for k in range(len(runs)):
+            bend(k)
+            if k > 0:
+                quantise_bent(k - 1)
+        quantise_bent(len(runs) - 1)
 
         h = [kept("h%d" % n, [P, S], F32) for n in range(8)]
         v_planes = (v_sc, v_sc1)
-        for n in range(8):
+        def second_product(n, j0, widths, tag):
             r_cols = slice(n * P, (n + 1) * P)
-            for half in range(2):
-                cols = slice(half * BANK, (half + 1) * BANK)
-                acc = bank("h_acc%d_%d" % (n, half), "ab"[half])
-                for a in range(2):
+            acc = bank("h_acc%d_%d" % (n, j0), tag)
+            starts = [sum(widths[:k]) for k in range(len(widths))]
+            for a in range(2):
+                for o, w in zip(starts, widths):
+                    cols = slice(j0 + o, j0 + o + w)
                     nc.tensor.matmul_mx(
-                        out=acc[:],
+                        out=acc[:, o : o + w],
                         lhsT=w3_c[:, a, 2 * n * P : 2 * (n + 1) * P].bitcast(FP4X4),
                         lhsT_scale=w_sc[:, a, r_cols],
                         rhs=v_c[a][:, cols].bitcast(FP8X4), rhs_scale=v_planes[a][:, cols],
-                        start=(a == 0), stop=False)
+                        start=(a == 0 and o == 0), stop=False)
+            for o, w in zip(starts, widths):
+                cols = slice(j0 + o, j0 + o + w)
                 nc.tensor.matmul_mx(
-                    out=acc[:],
+                    out=acc[:, o : o + w],
                     lhsT=w2_c[:, r_cols].bitcast(FP8X4), lhsT_scale=w_sc[4:P, 0, r_cols],
                     rhs=bent_c[:, cols].bitcast(FP8X4), rhs_scale=bent_sc[:, cols],
-                    start=False, stop=True)
-                nc.scalar.copy(h[n][:, cols], acc[:])
+                    start=False, stop=(o == starts[-1]))
+            nc.scalar.copy(h[n][:, j0 : j0 + sum(widths)], acc[:, 0 : sum(widths)])
 
-        w4_c = {(b, 0): kept("w4_c%d" % b, [P, KP], U32) for b in range(2)}
+        second_product(0, 0, [BANK], "a")
+        second_product(0, BANK, [CH] * 3, "b")
+        second_product(0, S - CH, [CH], "b")
+        for n in range(1, 8):
+            for half in range(2):
+                second_product(n, half * BANK, [BANK], "ab"[half])
+
+        w4_c = [kept("w4_c0", [P, 2, KP], U32)]
         w4_sc = kept("w4_sc", [P, 2, H], U8)
         w4_bf = {}
         for g in range(2):
             for b in range(2):
-                w4_bf[b, g] = staged("w4_bf%d%d" % (b, g), "bf", 6, [P, PACK * KP], BF16)
+                w4_bf[b, g] = staged("w4_bf%d%d" % (b, g), "bf", 5, [P, PACK * KP], BF16)
                 for q0 in range(0, P, 32):
                     deal_round(nc.scalar.copy, w4_bf[b, g], w4_raw[b, g], q0, q0 + 32)
             if g == 0:
                 load_base(1)
 
         def quantise_w4(b, g):
-            quantise(w4_c[b, g][:], w4_sc[:, b, g * KP : (g + 1) * KP], w4_bf[b, g][:])
+            quantise(w4_c[g][:, b, :], w4_sc[:, b, g * KP : (g + 1) * KP], w4_bf[b, g][:])
 
         def interleave_round(copy, dst, src):
             copy(dst.rearrange("p (c i t) -> p c t i", i=4, t=PACK),
@@ -248,7 +264,8 @@ def tile_list_seat_zone_asymmetry_kernel(
         right = {}
 
         def pick_right(n):
-            right[n] = staged("right%d" % n, "right", 2, [P, Z], F32)
+            tag, bufs = ("late", 1) if n == 7 else ("right", 2)
+            right[n] = staged("right%d" % n, tag, bufs, [P, Z], F32)
             nc.vector.tensor_copy(right[n][:], h[n][:].indirect(pos2_sb[:]))
 
         def subtract(n):
@@ -256,7 +273,7 @@ def tile_list_seat_zone_asymmetry_kernel(
                                     right[n][:], ALU.subtract)
 
         def round_x(b):
-            x_bf[b] = staged("x_bf%d" % b, "bf", 6, [P, PACK * Z], BF16)
+            x_bf[b] = staged("x_bf%d" % b, "late", 1, [P, PACK * Z], BF16)
             interleave_round(nc.scalar.copy, x_bf[b][:], x_f[b][:])
 
         pick_right(0)
@@ -270,12 +287,12 @@ def tile_list_seat_zone_asymmetry_kernel(
                 quantise_w4(1, 0)
                 quantise(x_c[:, 0, :], x_sc[:, 0, :], x_bf[0][:])
         subtract(7)
-        x_bf[1] = staged("x_bf1", "bf", 6, [P, PACK * Z], BF16)
+        x_bf[1] = staged("x_bf1", "bf", 5, [P, PACK * Z], BF16)
         interleave_round(nc.scalar.copy, x_bf[1][:, PACK * SPLIT :], x_f[1][:, :, SPLIT:])
         interleave_round(nc.vector.tensor_copy, x_bf[1][:, : PACK * SPLIT], x_f[1][:, :, :SPLIT])
         quantise(x_c[:, 1, :], x_sc[:, 1, :], x_bf[1][:])
+        w4_c.append(staged("w4_c1", "late", 1, [P, 2, KP], U32))
         for b in range(2):
-            w4_c[b, 1] = staged("w4_c%d1" % b, "right", 2, [P, KP], U32)
             quantise_w4(b, 1)
 
         for n in range(8):
@@ -284,7 +301,7 @@ def tile_list_seat_zone_asymmetry_kernel(
             for b in range(2):
                 nc.tensor.matmul_mx(
                     out=acc[:],
-                    lhsT=w4_c[b, n // PACK][:, (n % PACK) * P : (n % PACK + 1) * P].bitcast(FP8X4),
+                    lhsT=w4_c[n // PACK][:, b, (n % PACK) * P : (n % PACK + 1) * P].bitcast(FP8X4),
                     lhsT_scale=w4_sc[:, b, n_cols],
                     rhs=x_c[:, b, :].bitcast(FP8X4), rhs_scale=x_sc[:, b, :],
                     start=(b == 0), stop=(b == 1))
@@ -302,14 +319,14 @@ def tile_list_seat_zone_asymmetry_kernel(
         def raise_zone(s):
             g, j0, w, t = steps[s]
             n = PACK * g + t
-            raised[s] = staged("raised%d" % s, "raised", 5, [P, w], F32)
+            raised[s] = staged("raised%d" % s, "raised", 4, [P, w], F32)
             nc.vector.tensor_tensor(raised[s][:], zone[n][:].indirect(pos3_sb[:, j0 // 16 : (j0 + w) // 16]),
                                     h[n][:, j0 : j0 + w], ALU.mult)
 
         def add_base(s):
             g, j0, w, t = steps[s]
             dst = y[g][:, t, j0 : j0 + w]
-            if g == 1:
+            if s >= TURNED_STEPS:
                 nc.vector.tensor_tensor(dst, raised[s][:], dst, ALU.add)
                 return
             blocks = [slice(k * P, (k + 1) * P) for k in range(w // P)]
@@ -331,7 +348,7 @@ def tile_list_seat_zone_asymmetry_kernel(
             g, j0, w = pieces[k]
             cols = slice(j0, j0 + w)
             nc.sync.dma_start(out_rows[g][:, :, cols], y[g][:, :, cols])
-            y_bf[k] = staged("y_bf%d" % k, "bf", 6, [P, PACK * w], BF16)
+            y_bf[k] = staged("y_bf%d" % k, "bf", 5, [P, PACK * w], BF16)
             copy = nc.vector.tensor_copy if k == len(pieces) - 1 else nc.scalar.copy
             interleave_round(copy, y_bf[k][:], y[g][:, :, cols])
 

@@ -24,7 +24,7 @@ BANK = 512
 CH = 128
 SPARE = 16
 SPLIT = 352
-TURNED_STEPS = 11
+TURNED_STEPS = 9
 
 
 def tile_list_seat_zone_asymmetry_kernel(
@@ -47,12 +47,12 @@ def tile_list_seat_zone_asymmetry_kernel(
         def bank(name, tag):
             return psum.tile([P, BANK], F32, name=name, tag=tag)
 
-        tab_sc = staged("tab_sc", "bf", 5, [P, T], U8)
+        tab_sc = staged("tab_sc", "bf", 6, [P, T], U8)
         w_sc_raw = kept("w_sc_raw", [P, 2, H], U8)
-        v_sc1 = kept("v_sc1", [P, S], U8)
+        v_sc = kept("v_sc", [P, 2, S], U8)
         for plane in (tab_sc, w_sc_raw):
             nc.vector.memset(plane[:].bitcast(I32), 0)
-        nc.gpsimd.memset(v_sc1[:].bitcast(I32), 0)
+        nc.gpsimd.memset(v_sc[:].bitcast(I32), 0)
         ident = kept("ident", [P, P], F32)
         make_identity(nc, ident[:])
         zone = [kept("zone%d" % n, [P, Z + SPARE], F32) for n in range(8)]
@@ -63,7 +63,7 @@ def tile_list_seat_zone_asymmetry_kernel(
         pos1_sb = lists.tile([P, Z // 16], U16, name="pos1_sb")
         pos2_sb = lists.tile([P, Z // 16], U16, name="pos2_sb")
         pos3_sb = lists.tile([P, S // 16], U16, name="pos3_sb")
-        w3_raw = [staged("w3_raw%d" % a, "bf", 5, [P, 2 * H], U8) for a in range(2)]
+        w3_raw = [staged("w3_raw%d" % a, "bf", 6, [P, 2 * H], U8) for a in range(2)]
         for a in range(2):
             nc.sync.dma_start(w3_raw[a][:].bitcast(I32), w3_words[a].bitcast(I32))
         nc.sync.dma_start(offs_sb[:], offs)
@@ -74,39 +74,33 @@ def tile_list_seat_zone_asymmetry_kernel(
         nc.sync.dma_start(pos3_sb[:], pos3)
         tab = [staged("tab%d" % a, "big", 2, [P, T], I32) for a in range(2)]
 
-        def load_table(a, half):
-            cols = slice(half * T // 2, (half + 1) * T // 2)
+        def load_table(a, cols):
             nc.sync.dma_start(tab[a][:, cols], tab_words[a].rearrange("p t i -> p (t i)").bitcast(I32)[:, cols])
 
-        def load_tab_scales(q):
-            nc.sync.dma_start(tab_sc[32 * q : 32 * q + 8, :].bitcast(I32),
-                              tab_scales[:, 4 * q : 4 * q + 4, :].bitcast(I32))
+        def load_w3_scales(r):
+            nc.sync.dma_start(w_sc_raw[r:P:32, :, :].bitcast(I32),
+                              w3_scales[:, r:16:4, :].rearrange("a q n -> q a n").bitcast(I32))
 
-        def load_w3_scales(q):
-            nc.sync.dma_start(w_sc_raw[32 * q : 32 * q + 4, :, :].bitcast(I32),
-                              w3_scales[:, 4 * q : 4 * q + 4, :].rearrange("a r n -> r a n").bitcast(I32))
-
-        def load_w2_scales(q):
-            nc.sync.dma_start(w_sc_raw[32 * q + 4 : 32 * q + 8, 0, :].bitcast(I32),
-                              w2_scales[0, 4 * q : 4 * q + 4, :].bitcast(I32))
+        def load_w2_scales(r):
+            nc.sync.dma_start(w_sc_raw[4 + r : P : 32, 0, :].bitcast(I32), w2_scales[0, r:16:4, :].bitcast(I32))
 
         w1_rows = w1.rearrange("(a p i) m -> a p i m", p=P, i=PACK)
-        w1_raw = [staged("w1_raw%d" % a, "w4_raw", 4, [P, PACK, KP], F32) for a in range(2)]
+        w1_raw = [staged("w1_raw%d" % a, "x_f", 2, [P, PACK, KP], F32) for a in range(2)]
         for a in range(2):
             nc.sync.dma_start(w1_raw[a][:], w1_rows[a])
-        for q in range(4):
-            load_tab_scales(q)
-        load_table(0, 0)
-        load_w3_scales(0)
-        load_w3_scales(1)
-        load_table(0, 1)
-        load_w3_scales(2)
+        nc.sync.dma_start(tab_sc[0:P:4, :].bitcast(I32), tab_scales.rearrange("a q n -> q a n").bitcast(I32))
+        for r in range(3):
+            load_w3_scales(r)
+        load_table(0, slice(0, T // 2))
         load_w3_scales(3)
         load_w2_scales(0)
-        load_table(1, 0)
-        for q in range(1, 4):
-            load_w2_scales(q)
-        load_table(1, 1)
+        load_table(0, slice(T // 2, T))
+        for r in range(1, 4):
+            load_w2_scales(r)
+        load_table(1, slice(0, T // 2))
+        load_table(1, slice(T // 2, T))
+        back_sb = kept("back_sb", [P, 2, PACK], F32)
+        nc.sync.dma_start(back_sb[:], back.rearrange("(g p t) -> p g t", p=P, t=PACK))
 
         w3_c = kept("w3_c", [P, 2, 2 * H], U8)
         for a in range(2):
@@ -123,15 +117,17 @@ def tile_list_seat_zone_asymmetry_kernel(
 
         w1_c = kept("w1_c", [P, 2, M], U32)
         w1_sc = kept("w1_sc", [P, 2, M], U8)
-        w1_bf = [staged("w1_bf%d" % a, "bf", 5, [P, PACK * KP], BF16) for a in range(2)]
+        w1_bf = [staged("w1_bf%d" % a, "bf", 6, [P, PACK * KP], BF16) for a in range(2)]
         for a in range(2):
             deal_round(nc.scalar.copy, w1_bf[a], w1_raw[a][:], 0, P)
 
-        v_sc = kept("v_sc", [P, S], U8)
+        v_pick = kept("v_pick", [P, S], U8)
         v_c = [kept("v_c%d" % a, [P, S], U32) for a in range(2)]
         quantise(w1_c[:, 0, :], w1_sc[:, 0, :], w1_bf[0][:])
-        nc.vector.tensor_copy(v_sc[:], tab_sc[:].indirect(offs_sb[:]))
-        nc.sync.dma_start(v_sc1[0 : P - 4, :].bitcast(I32), v_sc[4:P, :].bitcast(I32))
+        nc.vector.tensor_copy(v_pick[:], tab_sc[:].indirect(offs_sb[:]))
+        for q in (0, 2, 1, 3):
+            nc.scalar.dma_start(v_sc[32 * q : 32 * q + 4, :, :].bitcast(I32),
+                                v_pick[32 * q : 32 * q + 32 : 4, :].bitcast(I32))
         quantise(w1_c[:, 1, :], w1_sc[:, 1, :], w1_bf[1][:])
         nc.vector.tensor_copy(v_c[0][:], tab[0][:].bitcast(U32).indirect(offs_sb[:]))
         w_sc = kept("w_sc", [P, 2, H], U8)
@@ -142,7 +138,7 @@ def tile_list_seat_zone_asymmetry_kernel(
         for half in range(2):
             nc.vector.tensor_copy(v_c[1][:, half * 512 : (half + 1) * 512],
                                   tab[1][:].bitcast(U32).indirect(offs_sb[:, half * 32 : (half + 1) * 32]))
-        w2_raw = staged("w2_raw", "bf", 5, [P, H], I32)
+        w2_raw = staged("w2_raw", "bf", 6, [P, H], I32)
         nc.sync.dma_start(w2_raw[:], w2_words[0].rearrange("p c i -> p (c i)").bitcast(I32))
         w2_c = kept("w2_c", [P, H], U32)
         nc.vector.tensor_copy(
@@ -151,12 +147,10 @@ def tile_list_seat_zone_asymmetry_kernel(
         w4_rows = w4.rearrange("(b p i) n -> b p i n", p=P, i=PACK)
         w4_raw = {}
         for g in range(2):
+            raw = staged("w4_raw%d" % g, "big", 2, [P, 2, PACK, KP], F32)
             for b in range(2):
-                raw = staged("w4_raw%d%d" % (b, g), "w4_raw", 4, [P, PACK, KP], F32)
-                nc.sync.dma_start(raw[:], w4_rows[b][:, :, g * KP : (g + 1) * KP])
-                w4_raw[b, g] = raw[:]
-        back_sb = kept("back_sb", [P, 2, PACK], F32)
-        nc.sync.dma_start(back_sb[:], back.rearrange("(g p t) -> p g t", p=P, t=PACK))
+                nc.sync.dma_start(raw[:, b], w4_rows[b][:, :, g * KP : (g + 1) * KP])
+                w4_raw[b, g] = raw[:, b]
         base_rows = base.rearrange("(g p t) j -> g p t j", p=P, t=PACK)
         y = []
 
@@ -164,8 +158,6 @@ def tile_list_seat_zone_asymmetry_kernel(
             rows = staged("y%d" % g, "big", 2, [P, PACK, S], F32)
             nc.sync.dma_start(rows[:], base_rows[g])
             y.append(rows)
-
-        load_base(0)
 
         n_ch = S // CH
         pre = [bank("pre%d" % c, "ab"[c % 2]) for c in range(n_ch)]
@@ -177,7 +169,7 @@ def tile_list_seat_zone_asymmetry_kernel(
                 nc.tensor.matmul_mx(
                     out=pre[c][:, t * CH : (t + 1) * CH],
                     lhsT=w1_c[:, a, m_cols].bitcast(FP8X4), lhsT_scale=w1_sc[:, a, m_cols],
-                    rhs=v_c[a][:, cols].bitcast(FP8X4), rhs_scale=v_sc[4 * a : P, cols],
+                    rhs=v_c[a][:, cols].bitcast(FP8X4), rhs_scale=v_sc[:, a, cols],
                     start=(a == 0 and t == 0), stop=(a == 1 and t == PACK - 1))
 
         bent_c = staged("bent_c", "late", 1, [P, S], U32)
@@ -209,7 +201,7 @@ def tile_list_seat_zone_asymmetry_kernel(
         quantise_bent(len(runs) - 1)
 
         h = [kept("h%d" % n, [P, S], F32) for n in range(8)]
-        v_planes = (v_sc, v_sc1)
+
         def second_product(n, j0, widths, tag):
             r_cols = slice(n * P, (n + 1) * P)
             acc = bank("h_acc%d_%d" % (n, j0), tag)
@@ -221,7 +213,7 @@ def tile_list_seat_zone_asymmetry_kernel(
                         out=acc[:, o : o + w],
                         lhsT=w3_c[:, a, 2 * n * P : 2 * (n + 1) * P].bitcast(FP4X4),
                         lhsT_scale=w_sc[:, a, r_cols],
-                        rhs=v_c[a][:, cols].bitcast(FP8X4), rhs_scale=v_planes[a][:, cols],
+                        rhs=v_c[a][:, cols].bitcast(FP8X4), rhs_scale=v_sc[:, a, cols],
                         start=(a == 0 and o == 0), stop=False)
             for o, w in zip(starts, widths):
                 cols = slice(j0 + o, j0 + o + w)
@@ -244,11 +236,10 @@ def tile_list_seat_zone_asymmetry_kernel(
         w4_bf = {}
         for g in range(2):
             for b in range(2):
-                w4_bf[b, g] = staged("w4_bf%d%d" % (b, g), "bf", 5, [P, PACK * KP], BF16)
+                w4_bf[b, g] = staged("w4_bf%d%d" % (b, g), "bf", 6, [P, PACK * KP], BF16)
                 for q0 in range(0, P, 32):
                     deal_round(nc.scalar.copy, w4_bf[b, g], w4_raw[b, g], q0, q0 + 32)
-            if g == 0:
-                load_base(1)
+            load_base(g)
 
         def quantise_w4(b, g):
             quantise(w4_c[g][:, b, :], w4_sc[:, b, g * KP : (g + 1) * KP], w4_bf[b, g][:])
@@ -287,7 +278,7 @@ def tile_list_seat_zone_asymmetry_kernel(
                 quantise_w4(1, 0)
                 quantise(x_c[:, 0, :], x_sc[:, 0, :], x_bf[0][:])
         subtract(7)
-        x_bf[1] = staged("x_bf1", "bf", 5, [P, PACK * Z], BF16)
+        x_bf[1] = staged("x_bf1", "bf", 6, [P, PACK * Z], BF16)
         interleave_round(nc.scalar.copy, x_bf[1][:, PACK * SPLIT :], x_f[1][:, :, SPLIT:])
         interleave_round(nc.vector.tensor_copy, x_bf[1][:, : PACK * SPLIT], x_f[1][:, :, :SPLIT])
         quantise(x_c[:, 1, :], x_sc[:, 1, :], x_bf[1][:])
@@ -319,7 +310,7 @@ def tile_list_seat_zone_asymmetry_kernel(
         def raise_zone(s):
             g, j0, w, t = steps[s]
             n = PACK * g + t
-            raised[s] = staged("raised%d" % s, "raised", 4, [P, w], F32)
+            raised[s] = staged("raised%d" % s, "raised", 6, [P, w], F32)
             nc.vector.tensor_tensor(raised[s][:], zone[n][:].indirect(pos3_sb[:, j0 // 16 : (j0 + w) // 16]),
                                     h[n][:, j0 : j0 + w], ALU.mult)
 
@@ -337,7 +328,7 @@ def tile_list_seat_zone_asymmetry_kernel(
             for k, blk in enumerate(blocks):
                 nc.tensor.matmul(turned[:, blk], raised[s][:, blk], ident[:], is_transpose=True,
                                  start=False, stop=(k == len(blocks) - 1))
-            summed = staged("summed%d" % s, "summed", 3, [P, w], F32)
+            summed = staged("summed%d" % s, "summed", 4, [P, w], F32)
             nc.scalar.copy(summed[:], turned[:])
             upright = bank("upright%d" % s, "a")
             for blk in blocks:
@@ -348,7 +339,7 @@ def tile_list_seat_zone_asymmetry_kernel(
             g, j0, w = pieces[k]
             cols = slice(j0, j0 + w)
             nc.sync.dma_start(out_rows[g][:, :, cols], y[g][:, :, cols])
-            y_bf[k] = staged("y_bf%d" % k, "bf", 5, [P, PACK * w], BF16)
+            y_bf[k] = staged("y_bf%d" % k, "bf", 6, [P, PACK * w], BF16)
             copy = nc.vector.tensor_copy if k == len(pieces) - 1 else nc.scalar.copy
             interleave_round(copy, y_bf[k][:], y[g][:, :, cols])
 

@@ -19,12 +19,26 @@ ALU = mybir.AluOpType
 
 P = 128
 PACK = 4
-KP = 512
+KP = P * PACK
 BANK = 512
-CH = 128
+TILES = H // P
+CHUNK = BANK // PACK
 SPARE = 16
-SPLIT = 352
-TURNED_STEPS = 9
+X_ON_VECTOR = 352
+W4_STEP = 32
+
+RINGS = {
+    "small": 6,
+    "big": 2,
+    "rows": 2,
+    "tanh": 3,
+    "bent": 2,
+    "chain": 1,
+    "right": 2,
+    "raised": 4,
+    "summed": 3,
+    "y_bf": 2,
+}
 
 
 def tile_list_seat_zone_asymmetry_kernel(
@@ -41,13 +55,13 @@ def tile_list_seat_zone_asymmetry_kernel(
         def kept(name, shape, dtype):
             return keep.tile(shape, dtype, name=name, align_bytes=64)
 
-        def staged(name, tag, bufs, shape, dtype):
-            return stage.tile(shape, dtype, name=name, tag=tag, bufs=bufs, align_bytes=64)
+        def staged(name, ring, shape, dtype):
+            return stage.tile(shape, dtype, name=name, tag=ring, bufs=RINGS[ring], align_bytes=64)
 
-        def bank(name, tag):
-            return psum.tile([P, BANK], F32, name=name, tag=tag)
+        def bank(name, ring):
+            return psum.tile([P, BANK], F32, name=name, tag=ring)
 
-        tab_sc = staged("tab_sc", "bf", 6, [P, T], U8)
+        tab_sc = staged("tab_sc", "small", [P, T], U8)
         w_sc_raw = kept("w_sc_raw", [P, 2, H], U8)
         v_sc = kept("v_sc", [P, 2, S], U8)
         for plane in (tab_sc, w_sc_raw):
@@ -55,15 +69,15 @@ def tile_list_seat_zone_asymmetry_kernel(
         nc.gpsimd.memset(v_sc[:].bitcast(I32), 0)
         ident = kept("ident", [P, P], F32)
         make_identity(nc, ident[:])
-        zone = [kept("zone%d" % n, [P, Z + SPARE], F32) for n in range(8)]
-        for z in zone:
-            nc.gpsimd.memset(z[:, Z:], 0.0)
+        zone = [kept("zone%d" % n, [P, Z + SPARE], F32) for n in range(TILES)]
+        for zone_tile in zone:
+            nc.gpsimd.memset(zone_tile[:, Z:], 0.0)
 
         offs_sb = lists.tile([P, S // 16], U16, name="offs_sb")
         pos1_sb = lists.tile([P, Z // 16], U16, name="pos1_sb")
         pos2_sb = lists.tile([P, Z // 16], U16, name="pos2_sb")
         pos3_sb = lists.tile([P, S // 16], U16, name="pos3_sb")
-        w3_raw = [staged("w3_raw%d" % a, "bf", 6, [P, 2 * H], U8) for a in range(2)]
+        w3_raw = [staged("w3_raw%d" % a, "small", [P, 2 * H], U8) for a in range(2)]
         for a in range(2):
             nc.sync.dma_start(w3_raw[a][:].bitcast(I32), w3_words[a].bitcast(I32))
         nc.sync.dma_start(offs_sb[:], offs)
@@ -72,9 +86,10 @@ def tile_list_seat_zone_asymmetry_kernel(
         nc.sync.dma_start(pos2_sb[:], pos2)
         nc.sync.dma_start(pos1_sb[:], pos1)
         nc.sync.dma_start(pos3_sb[:], pos3)
-        tab = [staged("tab%d" % a, "big", 2, [P, T], I32) for a in range(2)]
+        tab = [staged("tab%d" % a, "big", [P, T], I32) for a in range(2)]
 
-        def load_table(a, cols):
+        def load_table(a, half):
+            cols = slice(half * T // 2, (half + 1) * T // 2)
             nc.sync.dma_start(tab[a][:, cols], tab_words[a].rearrange("p t i -> p (t i)").bitcast(I32)[:, cols])
 
         def load_w3_scales(r):
@@ -85,20 +100,20 @@ def tile_list_seat_zone_asymmetry_kernel(
             nc.sync.dma_start(w_sc_raw[4 + r : P : 32, 0, :].bitcast(I32), w2_scales[0, r:16:4, :].bitcast(I32))
 
         w1_rows = w1.rearrange("(a p i) m -> a p i m", p=P, i=PACK)
-        w1_raw = [staged("w1_raw%d" % a, "x_f", 2, [P, PACK, KP], F32) for a in range(2)]
+        w1_raw = [staged("w1_raw%d" % a, "rows", [P, PACK, M], F32) for a in range(2)]
         for a in range(2):
             nc.sync.dma_start(w1_raw[a][:], w1_rows[a])
         nc.sync.dma_start(tab_sc[0:P:4, :].bitcast(I32), tab_scales.rearrange("a q n -> q a n").bitcast(I32))
         for r in range(3):
             load_w3_scales(r)
-        load_table(0, slice(0, T // 2))
+        load_table(0, 0)
         load_w3_scales(3)
         load_w2_scales(0)
-        load_table(0, slice(T // 2, T))
+        load_table(0, 1)
         for r in range(1, 4):
             load_w2_scales(r)
-        load_table(1, slice(0, T // 2))
-        load_table(1, slice(T // 2, T))
+        load_table(1, 0)
+        load_table(1, 1)
         back_sb = kept("back_sb", [P, 2, PACK], F32)
         nc.sync.dma_start(back_sb[:], back.rearrange("(g p t) -> p g t", p=P, t=PACK))
 
@@ -108,26 +123,26 @@ def tile_list_seat_zone_asymmetry_kernel(
                 w3_c[:, a, :].bitcast(U16).rearrange("p (b t q) -> p b t q", b=2, t=PACK),
                 w3_raw[a][:].bitcast(U16).rearrange("p (b q t) -> p b t q", b=2, t=PACK))
 
-        def deal_round(copy, dst, raw, q0, q1):
-            copy(dst[:].rearrange("p (t u e i) -> p u i e t", t=PACK, e=2, i=PACK)[:, q0 // 2 : q1 // 2],
-                 raw.rearrange("p i (u e t) -> p u i e t", t=PACK, e=2)[:, q0 // 2 : q1 // 2])
+        def deal_and_round(dst, raw, q0, q1):
+            nc.scalar.copy(dst[:].rearrange("p (t u e i) -> p u i e t", t=PACK, e=2, i=PACK)[:, q0 // 2 : q1 // 2],
+                           raw.rearrange("p i (u e t) -> p u i e t", t=PACK, e=2)[:, q0 // 2 : q1 // 2])
 
-        def quantise(codes, scales, src):
-            nc.vector.quantize_mx(out=codes.bitcast(FP8X4), scales=scales, in_=src)
+        def quantise(words, plane, src):
+            nc.vector.quantize_mx(out=words.bitcast(FP8X4), scales=plane, in_=src)
 
         w1_c = kept("w1_c", [P, 2, M], U32)
         w1_sc = kept("w1_sc", [P, 2, M], U8)
-        w1_bf = [staged("w1_bf%d" % a, "bf", 6, [P, PACK * KP], BF16) for a in range(2)]
+        w1_bf = [staged("w1_bf%d" % a, "small", [P, PACK * M], BF16) for a in range(2)]
         for a in range(2):
-            deal_round(nc.scalar.copy, w1_bf[a], w1_raw[a][:], 0, P)
+            deal_and_round(w1_bf[a], w1_raw[a][:], 0, P)
 
         v_pick = kept("v_pick", [P, S], U8)
         v_c = [kept("v_c%d" % a, [P, S], U32) for a in range(2)]
         quantise(w1_c[:, 0, :], w1_sc[:, 0, :], w1_bf[0][:])
         nc.vector.tensor_copy(v_pick[:], tab_sc[:].indirect(offs_sb[:]))
-        for q in (0, 2, 1, 3):
-            nc.scalar.dma_start(v_sc[32 * q : 32 * q + 4, :, :].bitcast(I32),
-                                v_pick[32 * q : 32 * q + 32 : 4, :].bitcast(I32))
+        for quad in (0, 2, 1, 3):
+            nc.scalar.dma_start(v_sc[32 * quad : 32 * quad + 4, :, :].bitcast(I32),
+                                v_pick[32 * quad : 32 * quad + 32 : 4, :].bitcast(I32))
         quantise(w1_c[:, 1, :], w1_sc[:, 1, :], w1_bf[1][:])
         nc.vector.tensor_copy(v_c[0][:], tab[0][:].bitcast(U32).indirect(offs_sb[:]))
         w_sc = kept("w_sc", [P, 2, H], U8)
@@ -136,9 +151,9 @@ def tile_list_seat_zone_asymmetry_kernel(
                 w_sc[:, a, :].rearrange("p (b t q) -> p b t q", b=2, t=PACK),
                 w_sc_raw[:, a, :].rearrange("p (b q t) -> p b t q", b=2, t=PACK))
         for half in range(2):
-            nc.vector.tensor_copy(v_c[1][:, half * 512 : (half + 1) * 512],
-                                  tab[1][:].bitcast(U32).indirect(offs_sb[:, half * 32 : (half + 1) * 32]))
-        w2_raw = staged("w2_raw", "bf", 6, [P, H], I32)
+            nc.vector.tensor_copy(v_c[1][:, half * S // 2 : (half + 1) * S // 2],
+                                  tab[1][:].bitcast(U32).indirect(offs_sb[:, half * S // 32 : (half + 1) * S // 32]))
+        w2_raw = staged("w2_raw", "small", [P, H], I32)
         nc.sync.dma_start(w2_raw[:], w2_words[0].rearrange("p c i -> p (c i)").bitcast(I32))
         w2_c = kept("w2_c", [P, H], U32)
         nc.vector.tensor_copy(
@@ -147,87 +162,84 @@ def tile_list_seat_zone_asymmetry_kernel(
         w4_rows = w4.rearrange("(b p i) n -> b p i n", p=P, i=PACK)
         w4_raw = {}
         for g in range(2):
-            raw = staged("w4_raw%d" % g, "big", 2, [P, 2, PACK, KP], F32)
+            w4_half = staged("w4_raw%d" % g, "big", [P, 2, PACK, KP], F32)
             for b in range(2):
-                nc.sync.dma_start(raw[:, b], w4_rows[b][:, :, g * KP : (g + 1) * KP])
-                w4_raw[b, g] = raw[:, b]
+                nc.sync.dma_start(w4_half[:, b], w4_rows[b][:, :, g * KP : (g + 1) * KP])
+                w4_raw[b, g] = w4_half[:, b]
         base_rows = base.rearrange("(g p t) j -> g p t j", p=P, t=PACK)
         y = []
 
         def load_base(g):
-            rows = staged("y%d" % g, "big", 2, [P, PACK, S], F32)
-            nc.sync.dma_start(rows[:], base_rows[g])
-            y.append(rows)
+            y.append(staged("y%d" % g, "big", [P, PACK, S], F32))
+            nc.sync.dma_start(y[g][:], base_rows[g])
 
-        n_ch = S // CH
-        pre = [bank("pre%d" % c, "ab"[c % 2]) for c in range(n_ch)]
+        pre = [bank("pre%d" % c, "ab"[c % 2]) for c in range(S // CHUNK)]
 
         def first_product(c, a):
-            cols = slice(c * CH, (c + 1) * CH)
+            cols = slice(c * CHUNK, (c + 1) * CHUNK)
             for t in range(PACK):
-                m_cols = slice(t * P, (t + 1) * P)
+                places = slice(t * P, (t + 1) * P)
                 nc.tensor.matmul_mx(
-                    out=pre[c][:, t * CH : (t + 1) * CH],
-                    lhsT=w1_c[:, a, m_cols].bitcast(FP8X4), lhsT_scale=w1_sc[:, a, m_cols],
+                    out=pre[c][:, t * CHUNK : (t + 1) * CHUNK],
+                    lhsT=w1_c[:, a, places].bitcast(FP8X4), lhsT_scale=w1_sc[:, a, places],
                     rhs=v_c[a][:, cols].bitcast(FP8X4), rhs_scale=v_sc[:, a, cols],
                     start=(a == 0 and t == 0), stop=(a == 1 and t == PACK - 1))
 
-        bent_c = staged("bent_c", "late", 1, [P, S], U32)
+        bent_c = staged("bent_c", "chain", [P, S], U32)
         bent_sc = kept("bent_sc", [P, S], U8)
         runs = [(0, 2), (2, 2), (4, 2), (6, 1), (7, 1)]
         bent_bf = {}
 
-        def bend(k):
-            c0, count = runs[k]
-            th = staged("th%d" % k, "th", 3, [P, count * CH, PACK], F32)
+        def bend(run):
+            c0, count = runs[run]
+            tanh = staged("tanh%d" % run, "tanh", [P, count * CHUNK, PACK], F32)
             for c in range(c0, c0 + count):
                 first_product(c, 0)
                 first_product(c, 1)
-                nc.scalar.activation(th[:, (c - c0) * CH : (c - c0 + 1) * CH, :],
-                                     pre[c][:].rearrange("p (t n) -> p n t", t=PACK), ACT.Tanh)
-            bent_bf[k] = staged("bent_bf%d" % k, "bent_bf", 2, [P, count * CH, PACK], BF16)
-            nc.vector.tensor_tensor(bent_bf[k][:], th[:],
-                                    gain_sb[:].unsqueeze(1).to_broadcast([P, count * CH, PACK]), ALU.mult)
+                nc.scalar.activation(tanh[:, (c - c0) * CHUNK : (c - c0 + 1) * CHUNK, :],
+                                     pre[c][:].rearrange("p (t j) -> p j t", t=PACK), ACT.Tanh)
+            bent_bf[run] = staged("bent_bf%d" % run, "bent", [P, count * CHUNK, PACK], BF16)
+            nc.vector.tensor_tensor(bent_bf[run][:], tanh[:],
+                                    gain_sb[:].unsqueeze(1).to_broadcast([P, count * CHUNK, PACK]), ALU.mult)
 
-        def quantise_bent(k):
-            c0, count = runs[k]
-            cols = slice(c0 * CH, (c0 + count) * CH)
-            quantise(bent_c[:, cols], bent_sc[:, cols], bent_bf[k][:].rearrange("p n t -> p (n t)"))
+        def quantise_bent(run):
+            c0, count = runs[run]
+            cols = slice(c0 * CHUNK, (c0 + count) * CHUNK)
+            quantise(bent_c[:, cols], bent_sc[:, cols], bent_bf[run][:].rearrange("p j t -> p (j t)"))
 
-        for k in range(len(runs)):
-            bend(k)
-            if k > 0:
-                quantise_bent(k - 1)
+        for run in range(len(runs)):
+            bend(run)
+            if run > 0:
+                quantise_bent(run - 1)
         quantise_bent(len(runs) - 1)
 
-        h = [kept("h%d" % n, [P, S], F32) for n in range(8)]
+        h = [kept("h%d" % n, [P, S], F32) for n in range(TILES)]
 
-        def second_product(n, j0, widths, tag):
-            r_cols = slice(n * P, (n + 1) * P)
-            acc = bank("h_acc%d_%d" % (n, j0), tag)
-            starts = [sum(widths[:k]) for k in range(len(widths))]
+        def second_product(n, j0, widths, ring):
+            places = slice(n * P, (n + 1) * P)
+            acc = bank("h_acc%d_%d" % (n, j0), ring)
+            starts = [sum(widths[:i]) for i in range(len(widths))]
             for a in range(2):
-                for o, w in zip(starts, widths):
-                    cols = slice(j0 + o, j0 + o + w)
+                for start, width in zip(starts, widths):
+                    cols = slice(j0 + start, j0 + start + width)
                     nc.tensor.matmul_mx(
-                        out=acc[:, o : o + w],
-                        lhsT=w3_c[:, a, 2 * n * P : 2 * (n + 1) * P].bitcast(FP4X4),
-                        lhsT_scale=w_sc[:, a, r_cols],
+                        out=acc[:, start : start + width],
+                        lhsT=w3_c[:, a, 2 * n * P : 2 * (n + 1) * P].bitcast(FP4X4), lhsT_scale=w_sc[:, a, places],
                         rhs=v_c[a][:, cols].bitcast(FP8X4), rhs_scale=v_sc[:, a, cols],
-                        start=(a == 0 and o == 0), stop=False)
-            for o, w in zip(starts, widths):
-                cols = slice(j0 + o, j0 + o + w)
+                        start=(a == 0 and start == 0), stop=False)
+            for start, width in zip(starts, widths):
+                cols = slice(j0 + start, j0 + start + width)
                 nc.tensor.matmul_mx(
-                    out=acc[:, o : o + w],
-                    lhsT=w2_c[:, r_cols].bitcast(FP8X4), lhsT_scale=w_sc[4:P, 0, r_cols],
+                    out=acc[:, start : start + width],
+                    lhsT=w2_c[:, places].bitcast(FP8X4), lhsT_scale=w_sc[4:P, 0, places],
                     rhs=bent_c[:, cols].bitcast(FP8X4), rhs_scale=bent_sc[:, cols],
-                    start=False, stop=(o == starts[-1]))
+                    start=False, stop=(start == starts[-1]))
             nc.scalar.copy(h[n][:, j0 : j0 + sum(widths)], acc[:, 0 : sum(widths)])
 
         second_product(0, 0, [BANK], "a")
-        second_product(0, BANK, [CH] * 3, "b")
-        second_product(0, S - CH, [CH], "b")
-        for n in range(1, 8):
+        second_product(0, BANK, [CHUNK] * (PACK - 1), "b")
+        second_product(0, S - CHUNK, [CHUNK], "b")
+        for n in range(1, TILES):
             for half in range(2):
                 second_product(n, half * BANK, [BANK], "ab"[half])
 
@@ -236,123 +248,115 @@ def tile_list_seat_zone_asymmetry_kernel(
         w4_bf = {}
         for g in range(2):
             for b in range(2):
-                w4_bf[b, g] = staged("w4_bf%d%d" % (b, g), "bf", 6, [P, PACK * KP], BF16)
-                for q0 in range(0, P, 32):
-                    deal_round(nc.scalar.copy, w4_bf[b, g], w4_raw[b, g], q0, q0 + 32)
+                w4_bf[b, g] = staged("w4_bf%d%d" % (b, g), "small", [P, PACK * KP], BF16)
+                for q0 in range(0, P, W4_STEP):
+                    deal_and_round(w4_bf[b, g], w4_raw[b, g], q0, q0 + W4_STEP)
             load_base(g)
 
         def quantise_w4(b, g):
             quantise(w4_c[g][:, b, :], w4_sc[:, b, g * KP : (g + 1) * KP], w4_bf[b, g][:])
 
-        def interleave_round(copy, dst, src):
-            copy(dst.rearrange("p (c i t) -> p c t i", i=4, t=PACK),
-                 src.rearrange("p t (c i) -> p c t i", i=4))
+        def interleave_and_round(copy, dst, src):
+            copy(dst.rearrange("p (c e t) -> p c t e", e=4, t=PACK), src.rearrange("p t (c e) -> p c t e", e=4))
 
-        x_f = [staged("x_f%d" % b, "x_f", 2, [P, PACK, Z], F32) for b in range(2)]
+        x_f = [staged("x_f%d" % b, "rows", [P, PACK, Z], F32) for b in range(2)]
         x_c = kept("x_c", [P, 2, Z], U32)
         x_sc = kept("x_sc", [P, 2, Z], U8)
-        x_bf = {}
         right = {}
 
         def pick_right(n):
-            tag, bufs = ("late", 1) if n == 7 else ("right", 2)
-            right[n] = staged("right%d" % n, tag, bufs, [P, Z], F32)
+            right[n] = staged("right%d" % n, "chain" if n == TILES - 1 else "right", [P, Z], F32)
             nc.vector.tensor_copy(right[n][:], h[n][:].indirect(pos2_sb[:]))
 
         def subtract(n):
             nc.vector.tensor_tensor(x_f[n // PACK][:, n % PACK, :], h[n][:].indirect(pos1_sb[:]),
                                     right[n][:], ALU.subtract)
 
-        def round_x(b):
-            x_bf[b] = staged("x_bf%d" % b, "late", 1, [P, PACK * Z], BF16)
-            interleave_round(nc.scalar.copy, x_bf[b][:], x_f[b][:])
+        def differences(n0, n1):
+            for n in range(n0, n1):
+                pick_right(n)
+                subtract(n - 1)
 
         pick_right(0)
-        for n in range(1, 8):
-            pick_right(n)
-            subtract(n - 1)
-            if n == 4:
-                quantise_w4(0, 0)
-                round_x(0)
-            if n == 6:
-                quantise_w4(1, 0)
-                quantise(x_c[:, 0, :], x_sc[:, 0, :], x_bf[0][:])
-        subtract(7)
-        x_bf[1] = staged("x_bf1", "bf", 6, [P, PACK * Z], BF16)
-        interleave_round(nc.scalar.copy, x_bf[1][:, PACK * SPLIT :], x_f[1][:, :, SPLIT:])
-        interleave_round(nc.vector.tensor_copy, x_bf[1][:, : PACK * SPLIT], x_f[1][:, :, :SPLIT])
-        quantise(x_c[:, 1, :], x_sc[:, 1, :], x_bf[1][:])
-        w4_c.append(staged("w4_c1", "late", 1, [P, 2, KP], U32))
+        differences(1, PACK + 1)
+        quantise_w4(0, 0)
+        x_bf0 = staged("x_bf0", "chain", [P, PACK * Z], BF16)
+        interleave_and_round(nc.scalar.copy, x_bf0[:], x_f[0][:])
+        differences(PACK + 1, TILES - 1)
+        quantise_w4(1, 0)
+        quantise(x_c[:, 0, :], x_sc[:, 0, :], x_bf0[:])
+        differences(TILES - 1, TILES)
+        subtract(TILES - 1)
+        x_bf1 = staged("x_bf1", "small", [P, PACK * Z], BF16)
+        interleave_and_round(nc.scalar.copy, x_bf1[:, PACK * X_ON_VECTOR :], x_f[1][:, :, X_ON_VECTOR:])
+        interleave_and_round(nc.vector.tensor_copy, x_bf1[:, : PACK * X_ON_VECTOR], x_f[1][:, :, :X_ON_VECTOR])
+        quantise(x_c[:, 1, :], x_sc[:, 1, :], x_bf1[:])
+        w4_c.append(staged("w4_c1", "chain", [P, 2, KP], U32))
         for b in range(2):
             quantise_w4(b, 1)
 
-        for n in range(8):
-            n_cols = slice(n * P, (n + 1) * P)
+        for n in range(TILES):
+            g, t = divmod(n, PACK)
             acc = bank("z_acc%d" % n, "a")
             for b in range(2):
                 nc.tensor.matmul_mx(
                     out=acc[:],
-                    lhsT=w4_c[n // PACK][:, b, (n % PACK) * P : (n % PACK + 1) * P].bitcast(FP8X4),
-                    lhsT_scale=w4_sc[:, b, n_cols],
+                    lhsT=w4_c[g][:, b, t * P : (t + 1) * P].bitcast(FP8X4), lhsT_scale=w4_sc[:, b, n * P : (n + 1) * P],
                     rhs=x_c[:, b, :].bitcast(FP8X4), rhs_scale=x_sc[:, b, :],
                     start=(b == 0), stop=(b == 1))
-            nc.scalar.activation(zone[n][:, 0:Z], acc[:], ACT.Copy,
-                                 scale=back_sb[:, n // PACK, n % PACK : n % PACK + 1])
+            nc.scalar.activation(zone[n][:, 0:Z], acc[:], ACT.Copy, scale=back_sb[:, g, t : t + 1])
 
         out_rows = out_0.rearrange("(g p t) j -> g p t j", p=P, t=PACK)
         y_c = [kept("y_c%d" % g, [P, S], U32) for g in range(2)]
-        y_sc = [kept("y_sc%d" % g, [P, S], U8) for g in range(2)]
-        pieces = [(0, 0, 512), (0, 512, 512), (1, 0, 512), (1, 512, 256), (1, 768, 256)]
-        steps = [(g, j0, w, t) for g, j0, w in pieces for t in range(PACK)]
+        y_sc = kept("y_sc", [P, S], U8)
+        pieces = [(0, 0, 512), (1, 0, 512), (0, 512, 512), (1, 512, 256), (1, 768, 256)]
+        steps = [(g, j0, width, t) for g, j0, width in pieces for t in range(PACK)]
         raised = {}
         y_bf = {}
 
         def raise_zone(s):
-            g, j0, w, t = steps[s]
+            g, j0, width, t = steps[s]
             n = PACK * g + t
-            raised[s] = staged("raised%d" % s, "raised", 6, [P, w], F32)
-            nc.vector.tensor_tensor(raised[s][:], zone[n][:].indirect(pos3_sb[:, j0 // 16 : (j0 + w) // 16]),
-                                    h[n][:, j0 : j0 + w], ALU.mult)
+            ring = "summed" if s >= len(steps) - PACK else "raised"
+            raised[s] = staged("raised%d" % s, ring, [P, width], F32)
+            picks = pos3_sb[:, j0 // 16 : (j0 + width) // 16]
+            nc.vector.tensor_tensor(raised[s][:], zone[n][:].indirect(picks), h[n][:, j0 : j0 + width], ALU.mult)
 
         def add_base(s):
-            g, j0, w, t = steps[s]
-            dst = y[g][:, t, j0 : j0 + w]
-            if s >= TURNED_STEPS:
+            g, j0, width, t = steps[s]
+            dst = y[g][:, t, j0 : j0 + width]
+            if g == 1:
                 nc.vector.tensor_tensor(dst, raised[s][:], dst, ALU.add)
                 return
-            blocks = [slice(k * P, (k + 1) * P) for k in range(w // P)]
+            squares = [slice(i * P, (i + 1) * P) for i in range(width // P)]
             turned = bank("turned%d" % s, "b")
-            for k, blk in enumerate(blocks):
-                nc.tensor.matmul(turned[:, blk], dst[:, blk], ident[:], is_transpose=True,
-                                 start=(k == 0), stop=False)
-            for k, blk in enumerate(blocks):
-                nc.tensor.matmul(turned[:, blk], raised[s][:, blk], ident[:], is_transpose=True,
-                                 start=False, stop=(k == len(blocks) - 1))
-            summed = staged("summed%d" % s, "summed", 4, [P, w], F32)
+            for i, square in enumerate(squares):
+                nc.tensor.matmul(turned[:, square], dst[:, square], ident[:], is_transpose=True,
+                                 start=(i == 0), stop=False)
+            for i, square in enumerate(squares):
+                nc.tensor.matmul(turned[:, square], raised[s][:, square], ident[:], is_transpose=True,
+                                 start=False, stop=(i == len(squares) - 1))
+            summed = staged("summed%d" % s, "summed", [P, width], F32)
             nc.scalar.copy(summed[:], turned[:])
             upright = bank("upright%d" % s, "a")
-            for blk in blocks:
-                nc.tensor.transpose(upright[:, blk], summed[:, blk], ident[:])
+            for square in squares:
+                nc.tensor.transpose(upright[:, square], summed[:, square], ident[:])
             nc.scalar.copy(dst, upright[:])
 
-        def finish_rows(k):
-            g, j0, w = pieces[k]
-            cols = slice(j0, j0 + w)
+        def store_and_round(piece):
+            g, j0, width = pieces[piece]
+            cols = slice(j0, j0 + width)
             nc.sync.dma_start(out_rows[g][:, :, cols], y[g][:, :, cols])
-            y_bf[k] = staged("y_bf%d" % k, "bf", 6, [P, PACK * w], BF16)
-            copy = nc.vector.tensor_copy if k == len(pieces) - 1 else nc.scalar.copy
-            interleave_round(copy, y_bf[k][:], y[g][:, :, cols])
+            y_bf[piece] = staged("y_bf%d" % piece, "y_bf", [P, PACK * width], BF16)
+            copy = nc.vector.tensor_copy if piece == len(pieces) - 1 else nc.scalar.copy
+            interleave_and_round(copy, y_bf[piece][:], y[g][:, :, cols])
 
-        def finish_planes(k):
-            g, j0, w = pieces[k]
-            cols = slice(j0, j0 + w)
-            quantise(y_c[g][:, cols], y_sc[g][:, cols], y_bf[k][:])
-            nc.sync.dma_start(out_1[g].rearrange("p m t -> p (m t)").bitcast(I32)[:, cols], y_c[g][:, cols].bitcast(I32))
-            if j0 + w == S:
-                for q in range(4):
-                    queue = nc.scalar if g == 1 and q % 2 == 0 else nc.sync
-                    queue.dma_start(out_2[g, 4 * q : 4 * q + 4, :].bitcast(I32),
-                                    y_sc[g][32 * q : 32 * q + 4, :].bitcast(I32))
+        def quantise_and_store(piece):
+            g, j0, width = pieces[piece]
+            cols = slice(j0, j0 + width)
+            quantise(y_c[g][:, cols], y_sc[4 * g : P, cols], y_bf[piece][:])
+            nc.sync.dma_start(out_1[g].rearrange("p m t -> p (m t)").bitcast(I32)[:, cols],
+                              y_c[g][:, cols].bitcast(I32))
 
         raise_zone(0)
         for s in range(1, len(steps) + 1):
@@ -360,7 +364,11 @@ def tile_list_seat_zone_asymmetry_kernel(
                 raise_zone(s)
             add_base(s - 1)
             if s % PACK == 0:
-                finish_rows(s // PACK - 1)
+                store_and_round(s // PACK - 1)
                 if s > PACK:
-                    finish_planes(s // PACK - 2)
-        finish_planes(len(pieces) - 1)
+                    quantise_and_store(s // PACK - 2)
+        quantise_and_store(len(pieces) - 1)
+        for quad in range(4):
+            queue = nc.scalar if quad % 2 == 0 else nc.sync
+            queue.dma_start(out_2[:, 4 * quad : 4 * quad + 4, :].bitcast(I32),
+                            y_sc[32 * quad : 32 * quad + 8, :].bitcast(I32))

from contextlib import ExitStack

import concourse.mybir as mybir
from concourse.masks import make_identity

K, M, H, T, S, Z = 1024, 512, 1024, 4096, 1024, 512
FLOPS = 2 * (K * M * S + M * H * S + K * H * S + H * H * Z)

F32 = mybir.dt.float32
BF16 = mybir.dt.bfloat16
I32 = mybir.dt.int32
U32 = mybir.dt.uint32
U16 = mybir.dt.uint16
U8 = mybir.dt.uint8
FP8X4 = mybir.dt.float8_e4m3fn_x4
FP4X4 = mybir.dt.float4_e2m1fn_x4
ACT = mybir.ActivationFunctionType
ALU = mybir.AluOpType

P = 128
PACK = 4
KP = P * PACK
BANK = 512
TILES = H // P
CHUNK = BANK // PACK
SPARE = 16
X_ON_VECTOR = 352
W4_STEP = 32

RINGS = {
    "small": 6,
    "big": 2,
    "rows": 2,
    "tanh": 3,
    "bent": 2,
    "chain": 1,
    "right": 2,
    "raised": 4,
    "summed": 3,
    "y_bf": 2,
}


def tile_list_seat_zone_asymmetry_kernel(
    tc, tab_words, tab_scales, offs, pos1, pos2, pos3, w1, gain, w2_words, w2_scales,
    w3_words, w3_scales, w4, back, base, out_0, out_1, out_2,
):
    nc = tc.nc
    with ExitStack() as ctx:
        lists = ctx.enter_context(tc.tile_pool(name="lists", bufs=1))
        keep = ctx.enter_context(tc.tile_pool(name="keep", bufs=1))
        stage = ctx.enter_context(tc.tile_pool(name="stage", bufs=2))
        psum = ctx.enter_context(tc.psum_pool(name="psum", bufs=4))

        def kept(name, shape, dtype):
            return keep.tile(shape, dtype, name=name, align_bytes=64)

        def staged(name, ring, shape, dtype):
            return stage.tile(shape, dtype, name=name, tag=ring, bufs=RINGS[ring], align_bytes=64)

        def bank(name, ring):
            return psum.tile([P, BANK], F32, name=name, tag=ring)

        tab_sc = staged("tab_sc", "small", [P, T], U8)
        w_sc_raw = kept("w_sc_raw", [P, 2, H], U8)
        v_sc = kept("v_sc", [P, 2, S], U8)
        for plane in (tab_sc, w_sc_raw):
            nc.vector.memset(plane[:].bitcast(I32), 0)
        nc.gpsimd.memset(v_sc[:].bitcast(I32), 0)
        ident = kept("ident", [P, P], F32)
        make_identity(nc, ident[:])
        zone = [kept("zone%d" % n, [P, Z + SPARE], F32) for n in range(TILES)]
        for zone_tile in zone:
            nc.gpsimd.memset(zone_tile[:, Z:], 0.0)

        offs_sb = lists.tile([P, S // 16], U16, name="offs_sb")
        pos1_sb = lists.tile([P, Z // 16], U16, name="pos1_sb")
        pos2_sb = lists.tile([P, Z // 16], U16, name="pos2_sb")
        pos3_sb = lists.tile([P, S // 16], U16, name="pos3_sb")
        w3_raw = [staged("w3_raw%d" % a, "small", [P, 2 * H], U8) for a in range(2)]
        for a in range(2):
            nc.sync.dma_start(w3_raw[a][:].bitcast(I32), w3_words[a].bitcast(I32))
        nc.sync.dma_start(offs_sb[:], offs)
        gain_sb = kept("gain_sb", [P, PACK], F32)
        nc.sync.dma_start(gain_sb[:], gain.rearrange("(p t) -> p t", t=PACK))
        nc.sync.dma_start(pos2_sb[:], pos2)
        nc.sync.dma_start(pos1_sb[:], pos1)
        nc.sync.dma_start(pos3_sb[:], pos3)
        tab = [staged("tab%d" % a, "big", [P, T], I32) for a in range(2)]

        def load_table(a, half):
            cols = slice(half * T // 2, (half + 1) * T // 2)
            nc.sync.dma_start(tab[a][:, cols], tab_words[a].rearrange("p t i -> p (t i)").bitcast(I32)[:, cols])

        def load_w3_scales(r):
            nc.sync.dma_start(w_sc_raw[r:P:32, :, :].bitcast(I32),
                              w3_scales[:, r:16:4, :].rearrange("a q n -> q a n").bitcast(I32))

        def load_w2_scales(r):
            nc.sync.dma_start(w_sc_raw[4 + r : P : 32, 0, :].bitcast(I32), w2_scales[0, r:16:4, :].bitcast(I32))

        w1_rows = w1.rearrange("(a p i) m -> a p i m", p=P, i=PACK)
        w1_raw = [staged("w1_raw%d" % a, "rows", [P, PACK, M], F32) for a in range(2)]
        for a in range(2):
            nc.sync.dma_start(w1_raw[a][:], w1_rows[a])
        nc.sync.dma_start(tab_sc[0:P:4, :].bitcast(I32), tab_scales.rearrange("a q n -> q a n").bitcast(I32))
        for r in range(3):
            load_w3_scales(r)
        load_table(0, 0)
        load_w3_scales(3)
        load_w2_scales(0)
        load_table(0, 1)
        for r in range(1, 4):
            load_w2_scales(r)
        load_table(1, 0)
        load_table(1, 1)
        back_sb = kept("back_sb", [P, 2, PACK], F32)
        nc.sync.dma_start(back_sb[:], back.rearrange("(g p t) -> p g t", p=P, t=PACK))

        w3_c = kept("w3_c", [P, 2, 2 * H], U8)
        for a in range(2):
            nc.vector.tensor_copy(
                w3_c[:, a, :].bitcast(U16).rearrange("p (b t q) -> p b t q", b=2, t=PACK),
                w3_raw[a][:].bitcast(U16).rearrange("p (b q t) -> p b t q", b=2, t=PACK))

        def deal_and_round(dst, raw, q0, q1):
            nc.scalar.copy(dst[:].rearrange("p (t u e i) -> p u i e t", t=PACK, e=2, i=PACK)[:, q0 // 2 : q1 // 2],
                           raw.rearrange("p i (u e t) -> p u i e t", t=PACK, e=2)[:, q0 // 2 : q1 // 2])

        def quantise(words, plane, src):
            nc.vector.quantize_mx(out=words.bitcast(FP8X4), scales=plane, in_=src)

        w1_c = kept("w1_c", [P, 2, M], U32)
        w1_sc = kept("w1_sc", [P, 2, M], U8)
        w1_bf = [staged("w1_bf%d" % a, "small", [P, PACK * M], BF16) for a in range(2)]
        for a in range(2):
            deal_and_round(w1_bf[a], w1_raw[a][:], 0, P)

        v_pick = kept("v_pick", [P, S], U8)
        v_c = [kept("v_c%d" % a, [P, S], U32) for a in range(2)]
        quantise(w1_c[:, 0, :], w1_sc[:, 0, :], w1_bf[0][:])
        nc.vector.tensor_copy(v_pick[:], tab_sc[:].indirect(offs_sb[:]))
        for quad in (0, 2, 1, 3):
            nc.scalar.dma_start(v_sc[32 * quad : 32 * quad + 4, :, :].bitcast(I32),
                                v_pick[32 * quad : 32 * quad + 32 : 4, :].bitcast(I32))
        quantise(w1_c[:, 1, :], w1_sc[:, 1, :], w1_bf[1][:])
        nc.vector.tensor_copy(v_c[0][:], tab[0][:].bitcast(U32).indirect(offs_sb[:]))
        w_sc = kept("w_sc", [P, 2, H], U8)
        for a in (1, 0):
            nc.vector.tensor_copy(
                w_sc[:, a, :].rearrange("p (b t q) -> p b t q", b=2, t=PACK),
                w_sc_raw[:, a, :].rearrange("p (b q t) -> p b t q", b=2, t=PACK))
        for half in range(2):
            nc.vector.tensor_copy(v_c[1][:, half * S // 2 : (half + 1) * S // 2],
                                  tab[1][:].bitcast(U32).indirect(offs_sb[:, half * S // 32 : (half + 1) * S // 32]))
        w2_raw = staged("w2_raw", "small", [P, H], I32)
        nc.sync.dma_start(w2_raw[:], w2_words[0].rearrange("p c i -> p (c i)").bitcast(I32))
        w2_c = kept("w2_c", [P, H], U32)
        nc.vector.tensor_copy(
            w2_c[:].bitcast(I32).rearrange("p (b t q) -> p b q t", b=2, t=PACK),
            w2_raw[:].rearrange("p (b q t) -> p b q t", b=2, t=PACK))
        w4_rows = w4.rearrange("(b p i) n -> b p i n", p=P, i=PACK)
        w4_raw = {}
        for g in range(2):
            w4_half = staged("w4_raw%d" % g, "big", [P, 2, PACK, KP], F32)
            for b in range(2):
                nc.sync.dma_start(w4_half[:, b], w4_rows[b][:, :, g * KP : (g + 1) * KP])
                w4_raw[b, g] = w4_half[:, b]
        base_rows = base.rearrange("(g p t) j -> g p t j", p=P, t=PACK)
        y = []

        def load_base(g):
            y.append(staged("y%d" % g, "big", [P, PACK, S], F32))
            nc.sync.dma_start(y[g][:], base_rows[g])

        pre = [bank("pre%d" % c, "ab"[c % 2]) for c in range(S // CHUNK)]

        def first_product(c, a):
            cols = slice(c * CHUNK, (c + 1) * CHUNK)
            for t in range(PACK):
                places = slice(t * P, (t + 1) * P)
                nc.tensor.matmul_mx(
                    out=pre[c][:, t * CHUNK : (t + 1) * CHUNK],
                    lhsT=w1_c[:, a, places].bitcast(FP8X4), lhsT_scale=w1_sc[:, a, places],
                    rhs=v_c[a][:, cols].bitcast(FP8X4), rhs_scale=v_sc[:, a, cols],
                    start=(a == 0 and t == 0), stop=(a == 1 and t == PACK - 1))

        bent_c = staged("bent_c", "chain", [P, S], U32)
        bent_sc = kept("bent_sc", [P, S], U8)
        runs = [(0, 2), (2, 2), (4, 2), (6, 1), (7, 1)]
        bent_bf = {}

        def bend(run):
            c0, count = runs[run]
            tanh = staged("tanh%d" % run, "tanh", [P, count * CHUNK, PACK], F32)
            for c in range(c0, c0 + count):
                first_product(c, 0)
                first_product(c, 1)
                nc.scalar.activation(tanh[:, (c - c0) * CHUNK : (c - c0 + 1) * CHUNK, :],
                                     pre[c][:].rearrange("p (t j) -> p j t", t=PACK), ACT.Tanh)
            bent_bf[run] = staged("bent_bf%d" % run, "bent", [P, count * CHUNK, PACK], BF16)
            nc.vector.tensor_tensor(bent_bf[run][:], tanh[:],
                                    gain_sb[:].unsqueeze(1).to_broadcast([P, count * CHUNK, PACK]), ALU.mult)

        def quantise_bent(run):
            c0, count = runs[run]
            cols = slice(c0 * CHUNK, (c0 + count) * CHUNK)
            quantise(bent_c[:, cols], bent_sc[:, cols], bent_bf[run][:].rearrange("p j t -> p (j t)"))

        for run in range(len(runs)):
            bend(run)
            if run > 0:
                quantise_bent(run - 1)
        quantise_bent(len(runs) - 1)

        h = [kept("h%d" % n, [P, S], F32) for n in range(TILES)]

        def second_product(n, j0, widths, ring):
            places = slice(n * P, (n + 1) * P)
            acc = bank("h_acc%d_%d" % (n, j0), ring)
            starts = [sum(widths[:i]) for i in range(len(widths))]
            for a in range(2):
                for start, width in zip(starts, widths):
                    cols = slice(j0 + start, j0 + start + width)
                    nc.tensor.matmul_mx(
                        out=acc[:, start : start + width],
                        lhsT=w3_c[:, a, 2 * n * P : 2 * (n + 1) * P].bitcast(FP4X4), lhsT_scale=w_sc[:, a, places],
                        rhs=v_c[a][:, cols].bitcast(FP8X4), rhs_scale=v_sc[:, a, cols],
                        start=(a == 0 and start == 0), stop=False)
            for start, width in zip(starts, widths):
                cols = slice(j0 + start, j0 + start + width)
                nc.tensor.matmul_mx(
                    out=acc[:, start : start + width],
                    lhsT=w2_c[:, places].bitcast(FP8X4), lhsT_scale=w_sc[4:P, 0, places],
                    rhs=bent_c[:, cols].bitcast(FP8X4), rhs_scale=bent_sc[:, cols],
                    start=False, stop=(start == starts[-1]))
            nc.scalar.copy(h[n][:, j0 : j0 + sum(widths)], acc[:, 0 : sum(widths)])

        second_product(0, 0, [BANK], "a")
        second_product(0, BANK, [CHUNK] * (PACK - 1), "b")
        second_product(0, S - CHUNK, [CHUNK], "b")
        for n in range(1, TILES):
            for half in range(2):
                second_product(n, half * BANK, [BANK], "ab"[half])

        w4_c = [kept("w4_c0", [P, 2, KP], U32)]
        w4_sc = kept("w4_sc", [P, 2, H], U8)
        w4_bf = {}
        for g in range(2):
            for b in range(2):
                w4_bf[b, g] = staged("w4_bf%d%d" % (b, g), "small", [P, PACK * KP], BF16)
                for q0 in range(0, P, W4_STEP):
                    deal_and_round(w4_bf[b, g], w4_raw[b, g], q0, q0 + W4_STEP)
            load_base(g)

        def quantise_w4(b, g):
            quantise(w4_c[g][:, b, :], w4_sc[:, b, g * KP : (g + 1) * KP], w4_bf[b, g][:])

        def interleave_and_round(copy, dst, src):
            copy(dst.rearrange("p (c e t) -> p c t e", e=4, t=PACK), src.rearrange("p t (c e) -> p c t e", e=4))

        x_f = [staged("x_f%d" % b, "rows", [P, PACK, Z], F32) for b in range(2)]
        x_c = kept("x_c", [P, 2, Z], U32)
        x_sc = kept("x_sc", [P, 2, Z], U8)
        right = {}

        def pick_right(n):
            right[n] = staged("right%d" % n, "chain" if n == TILES - 1 else "right", [P, Z], F32)
            nc.vector.tensor_copy(right[n][:], h[n][:].indirect(pos2_sb[:]))

        def subtract(n):
            nc.vector.tensor_tensor(x_f[n // PACK][:, n % PACK, :], h[n][:].indirect(pos1_sb[:]),
                                    right[n][:], ALU.subtract)

        def differences(n0, n1):
            for n in range(n0, n1):
                pick_right(n)
                subtract(n - 1)

        pick_right(0)
        differences(1, PACK + 1)
        quantise_w4(0, 0)
        x_bf0 = staged("x_bf0", "chain", [P, PACK * Z], BF16)
        interleave_and_round(nc.scalar.copy, x_bf0[:], x_f[0][:])
        differences(PACK + 1, TILES - 1)
        quantise_w4(1, 0)
        quantise(x_c[:, 0, :], x_sc[:, 0, :], x_bf0[:])
        differences(TILES - 1, TILES)
        subtract(TILES - 1)
        x_bf1 = staged("x_bf1", "small", [P, PACK * Z], BF16)
        interleave_and_round(nc.scalar.copy, x_bf1[:, PACK * X_ON_VECTOR :], x_f[1][:, :, X_ON_VECTOR:])
        interleave_and_round(nc.vector.tensor_copy, x_bf1[:, : PACK * X_ON_VECTOR], x_f[1][:, :, :X_ON_VECTOR])
        quantise(x_c[:, 1, :], x_sc[:, 1, :], x_bf1[:])
        w4_c.append(staged("w4_c1", "chain", [P, 2, KP], U32))
        for b in range(2):
            quantise_w4(b, 1)

        for n in range(TILES):
            g, t = divmod(n, PACK)
            acc = bank("z_acc%d" % n, "a")
            for b in range(2):
                nc.tensor.matmul_mx(
                    out=acc[:],
                    lhsT=w4_c[g][:, b, t * P : (t + 1) * P].bitcast(FP8X4), lhsT_scale=w4_sc[:, b, n * P : (n + 1) * P],
                    rhs=x_c[:, b, :].bitcast(FP8X4), rhs_scale=x_sc[:, b, :],
                    start=(b == 0), stop=(b == 1))
            nc.scalar.activation(zone[n][:, 0:Z], acc[:], ACT.Copy, scale=back_sb[:, g, t : t + 1])

        out_rows = out_0.rearrange("(g p t) j -> g p t j", p=P, t=PACK)
        y_c = [kept("y_c%d" % g, [P, S], U32) for g in range(2)]
        y_sc = kept("y_sc", [P, S], U8)
        pieces = [(0, 0, 512), (1, 0, 512), (0, 512, 512), (1, 512, 256), (1, 768, 256)]
        steps = [(g, j0, width, t) for g, j0, width in pieces for t in range(PACK)]
        raised = {}
        y_bf = {}

        def raise_zone(s):
            g, j0, width, t = steps[s]
            n = PACK * g + t
            ring = "summed" if s >= len(steps) - PACK else "raised"
            raised[s] = staged("raised%d" % s, ring, [P, width], F32)
            picks = pos3_sb[:, j0 // 16 : (j0 + width) // 16]
            nc.vector.tensor_tensor(raised[s][:], zone[n][:].indirect(picks), h[n][:, j0 : j0 + width], ALU.mult)

        def add_base(s):
            g, j0, width, t = steps[s]
            dst = y[g][:, t, j0 : j0 + width]
            if g == 1:
                nc.vector.tensor_tensor(dst, raised[s][:], dst, ALU.add)
                return
            squares = [slice(i * P, (i + 1) * P) for i in range(width // P)]
            turned = bank("turned%d" % s, "b")
            for i, square in enumerate(squares):
                nc.tensor.matmul(turned[:, square], dst[:, square], ident[:], is_transpose=True,
                                 start=(i == 0), stop=False)
            for i, square in enumerate(squares):
                nc.tensor.matmul(turned[:, square], raised[s][:, square], ident[:], is_transpose=True,
                                 start=False, stop=(i == len(squares) - 1))
            summed = staged("summed%d" % s, "summed", [P, width], F32)
            nc.scalar.copy(summed[:], turned[:])
            upright = bank("upright%d" % s, "a")
            for square in squares:
                nc.tensor.transpose(upright[:, square], summed[:, square], ident[:])
            nc.scalar.copy(dst, upright[:])

        def store_and_round(piece):
            g, j0, width = pieces[piece]
            cols = slice(j0, j0 + width)
            nc.sync.dma_start(out_rows[g][:, :, cols], y[g][:, :, cols])
            y_bf[piece] = staged("y_bf%d" % piece, "y_bf", [P, PACK * width], BF16)
            copy = nc.vector.tensor_copy if piece == len(pieces) - 1 else nc.scalar.copy
            interleave_and_round(copy, y_bf[piece][:], y[g][:, :, cols])

        def quantise_and_store(piece):
            g, j0, width = pieces[piece]
            cols = slice(j0, j0 + width)
            quantise(y_c[g][:, cols], y_sc[4 * g : P, cols], y_bf[piece][:])
            nc.sync.dma_start(out_1[g].rearrange("p m t -> p (m t)").bitcast(I32)[:, cols],
                              y_c[g][:, cols].bitcast(I32))

        raise_zone(0)
        for s in range(1, len(steps) + 1):
            if s < len(steps):
                raise_zone(s)
            add_base(s - 1)
            if s % PACK == 0:
                store_and_round(s // PACK - 1)
                if s > PACK:
                    quantise_and_store(s // PACK - 2)
        quantise_and_store(len(pieces) - 1)
        for quad in range(4):
            queue = nc.scalar if quad % 2 == 0 else nc.sync
            queue.dma_start(out_2[:, 4 * quad : 4 * quad + 4, :].bitcast(I32),
                            y_sc[32 * quad : 32 * quad + 8, :].bitcast(I32))
